import numpy as np, ml_dtypes
CORES = [16,17,18,19,32,33,34,35]
N = 8
import mx_ref
BF = ml_dtypes.bfloat16
def gcols(t, e):
    v = np.concatenate([t.reshape(8, 16, -1, 4), np.zeros((8, 16, 1, 4), BF)], axis=2)
    return np.ascontiguousarray(np.stack([v[g][:, e[g]] for g in range(8)])).reshape(128, -1)
def cut(t, i, w=512):
    return t[:, w * i:w * i + w]
def pick(q, e):
    c = np.concatenate([q[0].reshape(128, -1, 4), np.zeros((128, 1, 4), np.uint8)], axis=1); s = np.concatenate([q[1], np.ones((16, 1), np.uint8)], axis=1)
    return (np.ascontiguousarray(c[:, e].reshape(128, -1)), np.ascontiguousarray(s[:, e]))
def join(*qs):
    return (np.concatenate([q[0] for q in qs], axis=1), np.concatenate([q[1] for q in qs], axis=1))
def put(q, e, v):
    c, s = q[0].reshape(128, -1, 4).copy(), q[1].copy(); c[:, e] = v[0].reshape(128, -1, 4); s[:, e] = v[1]
    return (c.reshape(128, -1), s)
def pk(c, s):
    return (np.ascontiguousarray(c), mx_ref.live(s))
def emit(q):
    return q[0], q[1]
def packed(v, rng):
    q = [mx_ref.quantize(np.ascontiguousarray(v[r])) for r in range(N)]
    return np.stack([a for a, b in q]), np.stack([mx_ref.plane(b, rng) for a, b in q])
def values_of_codes():
    e, c = np.zeros((128, 128, 4), np.float32), np.zeros((128, 2, 4), np.uint8)
    e[np.arange(128), np.arange(128), 0] = 1
    c[:127, :, 0] = np.arange(256).reshape(2, 128).T[:127]
    return mx_ref.matmul(mx_ref.quantize(e.reshape(128, 512).astype(BF)), (c.reshape(128, 8), np.full((16, 2), 127, np.uint8))).T.reshape(-1).astype(np.float64)
CODE_VALUE, SCALE_VALUE = values_of_codes(), 2.0 ** (np.arange(256) - 127.0)
def decode(q):
    return (CODE_VALUE[q[0]].reshape(16, 8, -1, 4) * SCALE_VALUE[q[1]][:, None, :, None] + 0.0).reshape(128, -1).astype(np.float32)
def f(rng, *shape):
    return mx_ref.flush((rng.standard_normal(shape, dtype=np.float32) * np.exp2(rng.integers(-2, 3, shape[:-1] + (1,)))).astype(BF))
def wide(rng, *shape, cols=0):
    v = rng.standard_normal(shape, dtype=np.float32) * np.exp2(rng.integers(-12, 13, shape)).astype(np.float32)
    if cols: v *= np.repeat(np.exp2(rng.integers(-cols, cols + 1, shape[:-2] + (1, shape[-1] // 4))) * (rng.random(shape[:-2] + (1, shape[-1] // 4)) > 0.0625), 4, axis=-1).astype(np.float32)
    return mx_ref.flush(v.astype(BF))
C, M, L, T = 320, 512, 9, 3
def two(i):
    return np.arange(2 * C * i, 2 * C * i + 2 * C)
def product(a, q):
    return np.concatenate([mx_ref.matmul(a, pick(q, two(i))) for i in range(N // 2)], axis=1)
def unpacked(q):
    return np.concatenate([decode(pick(q, two(i))) for i in range(N // 2)], axis=1)
def place(a):
    e = np.full((8, M), C)
    np.minimum.at(e, (np.arange(8)[:, None], a), np.arange(C)[None, :])
    return np.where(e < C, M + e, np.arange(M)[None, :])
def same(a):
    return np.stack([a] * N)
def weights(rng, w):
    c, p = packed(same(w), rng)
    return {"wc": c, "ws": p}
def numbers_of(rng):
    return {"x": np.array(f(rng, N, 128, 4 * C)), "m": np.array(f(rng, N, 128, 4 * M))}
def digits(e, size):
    v = np.zeros(e.shape + (32,))
    v[..., :L] = (((e[..., None] >> np.arange(L)) & 1) * 2 - 1) * size[None, :, None, None]
    return np.moveaxis(v.reshape(e.shape + (8, 4)), 2, 3).astype(np.float32).astype(BF)
def setup_inputs(rng):
    return {**numbers_of(rng), "u": same(f(rng, 128, 512)), **weights(rng, f(rng, 128, 2048))}
def setup_inputs_ties(rng):
    d = numbers_of(rng)
    e = rng.permutation(N)
    x = d["x"].reshape(N, 8, 16, C, 4)
    for r in range(N):
        k = rng.permutation(C)
        if r == e[0]: k = np.zeros(C, int)
        elif r == e[2]: k = np.where(k < 256, 0, 2)
        else: k = k % 3
        a = x[r][:, :8, :3].copy()
        a[:, :, 2] = 0
        x[r][:, :8] = a[:, :, k]
    x[e[1]] = 0
    u = np.array(f(rng, 128, 512)).reshape(8, 16, 128, 4)
    u[:, 8:] = 0
    w = np.array(f(rng, 128, 2048)).reshape(8, 16, 4, 8, 16, 4)
    w[:, 8:, :, :, :8] = 0
    return {"x": x.reshape(N, 128, 4 * C), "m": d["m"], "u": same(u.reshape(128, 512)), **weights(rng, w.reshape(128, 2048))}
def setup_inputs_crowd(rng):
    d = numbers_of(rng)
    for n in ("x", "m"):
        p = d[n].reshape(N, 128, -1, 4)
        p[:, 15] = 0
        p[:, 15, :, 0] = 1
        d[n] = p.reshape(N, 128, -1)
    u = np.array(f(rng, 128, 512)).reshape(128, 128, 4)
    k = rng.permutation(np.array([0, 0, 1, 2, 3, 5, 7, L]))
    h = np.flatnonzero(k == 0)
    for g in range(8):
        z = 16 * g + rng.permutation(L)[k[g]:]
        s = rng.integers(-1, 2, len(z)) if k[g] else np.full(len(z), int(g == h[0]))
        u[:, z] = 0
        u[15, z, 0] = s.astype(np.float32).astype(BF)
    w = np.array(f(rng, 128, 2048)).reshape(128, 4, 128, 4)
    w[:, :, 15] = 0
    return {**d, "u": same(u.reshape(128, 512)), **weights(rng, w.reshape(128, 2048))}
def setup_inputs_chain(rng):
    d = numbers_of(rng)
    s = rng.permutation(8) % 2 * 2 - 1
    size = np.where(s > 0, 2.0 ** 28, 2.0 ** -30)
    x, m = d["x"].reshape(N, 8, 16, C, 4), d["m"].reshape(N, 8, 16, M, 4)
    to = np.stack([[rng.permutation(M) for g in range(8)] for r in range(N)])
    at = np.stack([[rng.permutation(M)[:C] for g in range(8)] for r in range(N)])
    x[:, :, :8] = digits(at, size)
    m[:, :, :8] = digits(to, size)
    u = np.array(f(rng, 128, 512)).reshape(8, 16, 128, 4)
    for g in range(8):
        for i in range(L):
            u[:, :, 16 * g + i] = 0
            u[g, i // 4, 16 * g + i, i % 4] = 2.0 ** 30 if s[g] > 0 else 2.0 ** -30
    w = np.array(f(rng, 128, 2048)).reshape(8, 16, 4, 8, 16, 4)
    w[:, :8] = 0
    w[:, :, :, :, :8] = 0
    for g in rng.permutation(8)[:4]:
        z = (N, 8, M, 4)
        m[:, g, 8:] = (rng.integers(8, 16, z) * np.exp2(-1.0 * rng.integers(13, 22, z)) * rng.choice([-1.0, 1.0], z)).astype(np.float32).astype(BF)
        m[:, g, 8, :, 0] = 1.625
        x[:, g, 8, :, 0] = -0.6875
        w[:, :, :, g, 8:] = 0
        w[g, 8, 0, g, 8, 0] = -32
    return {"x": x.reshape(N, 128, 4 * C), "m": m.reshape(N, 128, 4 * M), "u": same(u.reshape(128, 512)), **weights(rng, w.reshape(128, 2048))}
def setup_inputs_spread(rng):
    d = setup_inputs(rng)
    d["x"] = wide(rng, N, 128, 4 * C, cols=6)
    d["m"] = wide(rng, N, 128, 4 * M, cols=6)
    return d
def check_inputs(d):
    b = []
    for k in ("x", "m", "u"):
        a = np.abs(d[k].astype(np.float32))
        if not (np.isfinite(a).all() and ((a == 0) | (a >= 2.0 ** -30) & (a <= 2.0 ** 30)).all()): b.append("a value of " + k)
    if (d["u"].astype(np.float32) != d["u"][:1].astype(np.float32)).any(): b.append("u differs between ranks")
    if (d["wc"] != d["wc"][:1]).any(): b.append("wc differs between ranks")
    s = [mx_ref.live(p) for p in d["ws"]]
    if any((p != s[0]).any() for p in s): b.append("ws differs between ranks")
    a = np.abs(decode(pk(d["wc"][0], d["ws"][0])))
    if ((d["wc"] & 127) == 127).any() or not ((a == 0) | (a >= 2.0 ** -30) & (a <= 2.0 ** 30)).all(): b.append("a value of W")
    return b
def reference(x, m, u, wc, ws):
    w, qu = pk(wc[0], ws[0]), mx_ref.quantize(u[0])
    part = [pick(w, np.arange(128 * b, 128 * b + 128)) for b in range(4)]
    state = join(*[mx_ref.quantize(x[r]) for r in range(N)])
    maps = [m[r] for r in range(N)]
    power = (1 << np.arange(L)).reshape(1, L, 1, 1)
    for t in range(T):
        a = product(qu, state).reshape(8, 16, N, C)
        at = np.sum((a[:, :L] > 0) * power, axis=1)
        reads = np.concatenate([gcols(maps[(r + t) % N], at[:, r]) for r in range(N)], axis=1)
        layer = np.stack([product(part[b], state) * np.float32(0.015625) for b in range(4)], axis=2).reshape(128, -1)
        state = mx_ref.quantize((layer + unpacked(mx_ref.quantize(reads))).astype(BF))
        new = unpacked(state).astype(BF)
        for r in range(N):
            h = (r + t) % N
            maps[h] = gcols(np.concatenate([maps[h], cut(new, r, 4 * C)], axis=1), place(at[:, r]))
    last = product(part[0], state)
    y = np.zeros((N, 128, C), np.float32)
    oc, osc = np.zeros((N, 128, 4 * (C + M)), np.uint8), np.zeros((N, 16, C + M), np.uint8)
    for r in range(N):
        y[r] = cut(last, r, C)
        oc[r], osc[r] = emit(join(pick(state, C * r + np.arange(C)), mx_ref.quantize(maps[r])))
    return {"y": y, "oc": oc, "osc": osc}

@@ -1,0 +1,400 @@
+from concourse.mybir import dt, AluOpType, AxisListType, ActivationFunctionType
+
+C, M, VISITS = 320, 512, 3
+CODES, U8, BF, F32, F16, U16, I32 = "float8_e4m3fn_x4", "uint8", "bfloat16", "float32", "float16", "uint16", "int32"
+O = {"dfirst": True, "pre": (4,), "mid": (3, 2), "mid0": (4, 3), "cut": 320, "bcut": 38, "on": "slc", "off": "slc", "ret": "csl"}
+
+
+def _sb(n, d):
+    return ("sbuf", [128, n], d)
+
+
+SCRATCH = {
+    "ut": _sb(512, BF), "uc": _sb(128, CODES), "us": _sb(128, U8),
+    "xt": _sb(4 * C, BF), "s0c": _sb(C, CODES), "s0s": _sb(C, U8),
+    "wcb": _sb(512, CODES), "wsb": _sb(512, U8),
+    "win": _sb(4 * (M + VISITS * C), BF),
+    "et": _sb(516, BF), "ec": _sb(512, CODES), "es": _sb(512, U8), "c64": _sb(128, BF),
+    "plt": _sb(512, BF), "plc": _sb(128, CODES), "pls": _sb(128, U8),
+    "pwt": _sb(560, BF), "pwc": _sb(140, CODES), "pws": _sb(140, U8),
+    "bits": _sb(524, BF), "bac": _sb(130, CODES), "bas": _sb(130, U8), "bbc": _sb(130, CODES), "bbs": _sb(130, U8),
+    "qi": _sb(1, I32), "ci": _sb(8, I32), "cf": _sb(8, F32), "i64": _sb(64, F32), "ip4": _sb(128, BF),
+    "mm": _sb(16, F32), "wr": _sb(4, F32), "wv": _sb(4, F32), "g4t": _sb(4, F32),
+    "k0": _sb(32, F32), "k1": _sb(512, BF), "k2": _sb(256, BF),
+    "iota": _sb(M + VISITS * C, F32), "ptab": _sb(768, F32),
+    "ls0": _sb(20, U16), "lo1": _sb(20, U16), "lo2": _sb(20, U16), "ls1": _sb(20, U16), "ls2": _sb(20, U16),
+    "gg": _sb(C, F16), "gs": _sb(C, F16), "off0": _sb(80, U16), "off1": _sb(80, U16), "off2": _sb(80, U16),
+    "bt": _sb(4 * C, BF), "bc": _sb(C, CODES), "bs": _sb(C, U8),
+    "yt": _sb(4 * C, BF),
+    "o1c": _sb(C, CODES), "o1s": _sb(C, U8), "o2c": _sb(C, CODES), "o2s": _sb(C, U8), "o3c": _sb(C, CODES), "o3s": _sb(C, U8),
+    "s1c": _sb(C, CODES), "s1s": _sb(C, U8), "s2c": _sb(C, CODES), "s2s": _sb(C, U8), "s3c": _sb(C, CODES),
+    "fs": _sb(C + M, U8), "fc": _sb(M, CODES), "mf": _sb(4 * M, BF),
+    "rep": _sb(C, F32), "negb": _sb(20, F32), "nega": _sb(20, F32),
+    "cmp": _sb(4 * C, BF), "scn": _sb(4 * C, BF), "mn": _sb(20, F32), "sco": _sb(20, U16),
+    "fsc": _sb(M, F32), "offm": _sb(128, U16), "yo": _sb(C, F32),
+    "py0": ("psum", [128, 512], F32), "py1": ("psum", [128, 512], F32), "py2": ("psum", [128, 512], F32),
+    "py3": ("psum", [128, 512], F32), "pa": ("psum", [128, 512], F32), "pl": ("psum", [128, 512], F32),
+    "pw": ("psum", [128, 512], F32), "pb": ("psum", [128, 512], F32),
+}
+REMOTE = ["ac1", "as1", "al1", "ac2", "as2", "al2", "ac3", "as3", "sent"]
+SEMAPHORES = REMOTE + ["z%d" % i for i in range(100)]
+
+OP, ACT = AluOpType, ActivationFunctionType
+
+
+def rank_program(g, core, T, topo):
+    rank = T.rank_of(core)
+    if rank is None:
+        return
+    n = len(T.cores)
+    V, S, P, Y = g.vector, g.scalar, g.tensor, g.sync
+    qname = {"V": V, "S": S, "P": P, "Y": Y, "G": g}
+    slot, cnt, seen, top = {}, {}, {}, {}
+
+    def sem(role):
+        if role in REMOTE:
+            return T.sem[role]
+        if role not in slot:
+            slot[role] = "z%d" % len(slot)
+        return T.sem[slot[role]]
+
+    def inc(instr, role, k=1):
+        instr.then_inc(sem(role), k)
+        cnt[role] = cnt.get(role, 0) + k
+        return (role, cnt[role])
+
+    def wait(q, *toks):
+        for role, val in toks:
+            if seen.get((q, role), 0) < val:
+                qname[q].wait_ge(sem(role), val)
+                seen[(q, role)] = val
+                top[role] = max(top.get(role, 0), val)
+
+    def ts(out, in0, s1, op0, s2=None, op1=None):
+        if op1 is None:
+            return V.tensor_scalar(out, in0, s1, None, op0)
+        return V.tensor_scalar(out, in0, s1, s2, op0, op1)
+
+    def quant(c, s, tile):
+        return V.quantize_mx(c, s, tile)
+
+    def send(dst, out, src, role):
+        rid, pid, _ = topo.addr(dst)
+        g.remote_dma(out, src, sem(role), sem("sent"), pid, rid, topo.mask(core, dst))
+        cnt["sent"] = cnt.get("sent", 0) + len(topo.engines(core, dst))
+
+    def arrival(src, role):
+        cnt[role] = len(topo.engines(src, core))
+        return (role, cnt[role])
+
+    nxt, prv = T.cores[(rank + 1) % n], T.cores[(rank - 1) % n]
+    home, away = T.cores[(rank - (VISITS - 1)) % n], T.cores[(rank + VISITS - 1) % n]
+
+    t_u = inc(S.dma_start(T.ut[:], T.u[:]), "ld_u", 16)
+    t_x = inc(Y.dma_start(T.xt[:], T.x[:]), "ld_x", 16)
+    t_m = inc(Y.dma_start(T.win[:, 0:4 * M], T.m[:]), "ld_m", 16)
+    inc(Y.dma_start(T.wcb[:].bitcast(dt.uint8), T.wc[:]), "ld_w", 16)
+    t_w = inc(Y.dma_start(T.wsb[:], T.ws[:]), "ld_w", 16)
+
+    t_qi = inc(g.iota(T.qi[:], [[0, 1]], 0, 1), "g_qi")
+    t_i64 = inc(g.iota(T.i64[:], [[1, 64]], 0, 0, allow_small_or_imprecise_dtypes=True), "g_i64")
+    t_ip4 = inc(g.iota(T.ip4[:], [[1, 32], [0, 4]], 0, 0, allow_small_or_imprecise_dtypes=True), "g_ip4")
+    inc(V.memset(T.c64[:], 64.0), "v_e0")
+    t_e0 = inc(V.memset(T.et[:], 0.0), "v_e0")
+    inc(V.memset(T.pwt[:], 0.0), "vc")
+    inc(V.memset(T.bits[:, C:524], 0.0), "vc")
+    wait("G", t_e0)
+    t_e = inc(g.affine_select(T.et[:, 3:515:4], T.c64[:], [[-1, 128]], OP.is_equal, 0.0, 0, 1), "g_e")
+    t_iota = inc(g.iota(T.iota[:, 0:M + C], [[1, M + C]], 0, 0, allow_small_or_imprecise_dtypes=True), "g_iota")
+
+    wait("V", t_qi)
+    inc(ts(T.ci[:, 0:1], T.qi[:], 15, OP.bitwise_and), "vc")
+    inc(ts(T.ci[:, 1:2], T.qi[:], 3, OP.bitwise_and), "vc")
+    inc(ts(T.ci[:, 2:3], T.qi[:], 2, OP.logical_shift_right, 3, OP.bitwise_and), "vc")
+    inc(ts(T.ci[:, 3:4], T.qi[:], 4, OP.logical_shift_right), "vc")
+    t = inc(ts(T.ci[:, 4:5], T.qi[:], 2, OP.logical_shift_right, 28, OP.bitwise_and), "vc")
+    wait("V", t)
+    t = inc(V.tensor_copy(T.cf[:, 0:5], T.ci[:, 0:5]), "vc")
+    lane, l4, sel, grp, grp4 = [T.cf[:, i:i + 1] for i in range(5)]
+    wait("V", t, t_i64)
+    inc(ts(T.mm[:, 0:9], T.i64[:, 0:9], lane, OP.is_lt, 1.0, OP.add), "vc")
+    inc(ts(T.k0[:, 2:3], sel, 1.0, OP.add), "vc")
+    t = inc(ts(T.g4t[:], T.i64[:, 0:4], grp4, OP.add), "vc")
+    wait("V", t)
+    inc(ts(T.k0[:, 4:8], T.i64[:, 0:4], sel, OP.is_equal, 4096.0, OP.mult), "vc")
+    inc(ts(T.k0[:, 8:12], T.i64[:, 0:4], T.k0[:, 2:3], OP.is_equal, -2048.0, OP.mult), "vc")
+    t = inc(V.tensor_reduce(T.wr[:, 0:1], T.mm[:, 0:9], AxisListType.X, OP.mult), "vc")
+    wait("V", t)
+    t_cm = inc(V.tensor_tensor(T.k0[:, 12:16], T.k0[:, 4:8], T.k0[:, 8:12], OP.add), "v_cm")
+    t = inc(ts(T.wv[:, 0:1], lane, 9.0, OP.is_lt, T.wr[:, 0:1], OP.mult), "vc")
+    wgt = T.wv[:, 0:1]
+    wait("V", t, t_ip4)
+    for k in range(4):
+        inc(ts(T.plt[:, k:512:4], T.ip4[:], T.g4t[:, k:k + 1], OP.is_equal, wgt, OP.mult), "vc")
+    for k in range(4):
+        inc(ts(T.pwt[:, 48 + 5 * k:560:64], T.i64[:, 0:8], grp, OP.is_equal, wgt, OP.mult), "vc")
+    inc(ts(T.k0[:, 0:1], sel, 3.0, OP.is_lt, 8192.0, OP.mult), "vc")
+    t = inc(ts(T.k0[:, 16:20], T.i64[:, 0:4], 16.0, OP.mult, lane, OP.add), "vc")
+    wait("V", t_u)
+    t_qu = inc(quant(T.uc[:], T.us[:], T.ut[:]), "q_u")
+    wait("V", t)
+    t_pl = inc(quant(T.plc[:], T.pls[:], T.plt[:]), "q_pl")
+    t_qpw = inc(quant(T.pwc[:], T.pws[:], T.pwt[:]), "q_pw")
+    inc(ts(T.k0[:, 1:2], T.k0[:, 0:1], l4, OP.add), "vc")
+    t_k0 = inc(ts(T.k0[:, 20:24], T.k0[:, 16:20], -4.0, OP.mult, -512.0, OP.add), "vc")
+    kc = {}
+    wait("S", t_cm, t_ip4)
+    for k in range(4):
+        kc["k1"] = inc(S.activation(T.k1[:, k:M:4], T.ip4[:], ACT.Identity, bias=T.k0[:, 12 + k:13 + k], scale=0.0), "s_k1")
+    wait("S", t_iota)
+    t_p0 = inc(S.activation(T.ptab[:, 0:M], T.iota[:, 0:M], ACT.Copy), "s_p0")
+
+    H = C // 2
+
+    def quant_halves(sc, ss, tile):
+        return [inc(quant(sc[:, H * i:H * i + H], ss[:, H * i:H * i + H], tile[:, 4 * H * i:4 * H * (i + 1)]), "q_y%d" % i) for i in range(2)]
+
+    def bits_of(sc, ss, ready):
+        ta = []
+        for i, bank in enumerate((T.pa, T.pb)):
+            wait("P", t_qu, ready[i])
+            ta.append(inc(P.matmul_mx(bank[:, 0:H], T.uc[:], T.us[:], sc[:, H * i:H * i + H], ss[:, H * i:H * i + H], True, True), "m_a%d" % i))
+        for i, bank in enumerate((T.pa, T.pb)):
+            wait("V", ta[i])
+            tb = inc(ts(T.bits[:, H * i:H * i + H], bank[:, 0:H], 0.0, OP.is_gt), "v_bits")
+        wait("V", tb)
+        return inc(quant(T.bac[:], T.bas[:], T.bits[:, 0:520]), "q_ba")
+
+    def second_bits():
+        return inc(quant(T.bbc[:], T.bbs[:], T.bits[:, 4:524]), "q_bb")
+
+    def list_products(tba, tbb):
+        for i, s in enumerate((0, 2, 1, 3)):
+            wait("P", t_qpw, tba if s % 2 == 0 else tbb)
+            bc, bs = (T.bac, T.bas) if s % 2 == 0 else (T.bbc, T.bbs)
+            a, o = 12 - 4 * s, s - s % 2
+            ins = P.matmul_mx(T.pw[:, 0:128], T.pwc[:, a:a + 128], T.pws[:, a:a + 128], bc[:, o:o + 128], bs[:, o:o + 128], i == 0, i == 3)
+        return inc(ins, "m_w")
+
+    wait("V", t_x)
+    t_s0 = quant_halves(T.s0c, T.s0s, T.xt)
+    tba = bits_of(T.s0c, T.s0s, t_s0)
+    wait("P", t_pl, tba)
+    t_l80 = inc(P.matmul_mx(T.pl[:, 0:128], T.plc[:], T.pls[:], T.bac[:, 0:128], T.bas[:, 0:128], True, True), "m_l")
+    tbb = second_bits()
+    wait("V", t_l80)
+    t_off = inc(ts(T.off0[:], T.pl[:, 0:80], 4.0, OP.mult, l4, OP.add), "v_off")
+    t_w16 = list_products(tba, tbb)
+    wait("V", t_e)
+    for b in range(4):
+        t_qe = inc(quant(T.ec[:, 128 * b:128 * b + 128], T.es[:, 128 * b:128 * b + 128], T.et[:, 3 - b:515 - b]), "q_e")
+    wait("V", t_w16)
+    t_ls = inc(V.tensor_copy(T.ls0[:], T.pw[:, 0:80:4]), "v_ls")
+
+    state = [(T.s0c, T.s0s, t_s0), (T.s1c, T.s1s, None), (T.s2c, T.s2s, None)]
+    outs = [(T.o1c, T.o1s), (T.o2c, T.o2s), (T.o3c, T.o3s)]
+    lands = [(T.s1c[:], T.s1s[:]), (T.s2c[:], T.s2s[:]), (T.s3c[:], T.fs[:, 0:C])]
+    lists, sent_lists, offs = [T.ls0, T.ls1, T.ls2], [T.lo1, T.lo2], [T.off0, T.off1, T.off2]
+    pys = [T.py0, T.py1, T.py2, T.py3]
+    t_z = t_tab = None
+
+    for v in range(VISITS):
+        last = v == VISITS - 1
+        sc, ss, ready = state[v]
+        ls, off = lists[v], offs[v]
+        oc_, os_ = outs[v]
+        wlen = 4 * (M + v * C)
+        if v > 0:
+            ready = [arrival(prv, "ac%d" % v), arrival(prv, "as%d" % v)]
+            t_ls = arrival(prv, "al%d" % v)
+            wait("V", t_ls, t_tab)
+            t = inc(V.tensor_copy(T.gg[:], T.ptab[:, 0:M].indirect(ls[:])), "v_g")
+            t_neg = inc(ts(T.negb[:], ls[:], -1024.0, OP.mult), "v_neg")
+            wait("V", t, kc["k1"])
+            t = inc(V.tensor_tensor_scan(T.gs[:], T.k1[:, 0:C], T.gg[:], 0.0, OP.add, OP.min), "v_g")
+            t_nega = inc(ts(T.nega[:], ls[:], -1.0, OP.mult), "v_nega")
+            wait("V", t)
+            t_off = inc(ts(off[:], T.gs[:, 3:C:4], 4.0, OP.mult, T.k0[:, 1:2], OP.add), "v_off")
+        t_cmp, scanned = {}, []
+
+        def addresses():
+            wait("S", t_ls, t_iota)
+            if v > 0:
+                wait("S", kc["cmp"])
+            wait("S", inc(S.activation(T.rep[:], T.iota[:, 0:M].indirect(ls[:]), ACT.Copy), "s_rep"), t_neg)
+
+        def compare(blocks):
+            for b in blocks:
+                for k in range(4 * b, 4 * b + 4):
+                    t_cmp[b] = inc(S.activation(T.cmp[:, 64 * k:64 * k + 64], T.rep[:, 64 * b:64 * b + 64], ACT.Abs, bias=T.negb[:, k:k + 1], scale=1024.0), "s_c%d" % b)
+
+        def scans(blocks):
+            wait("V", kc["k2"])
+            for b in blocks:
+                wait("V", t_cmp[b])
+                scanned.append(b)
+                kc["scan"] = inc(V.tensor_tensor_scan(T.scn[:, 256 * b:256 * b + 256], T.k2[:], T.cmp[:, 256 * b:256 * b + 256], 0.0, OP.add, OP.min), "v_s")
+
+        def layer(b, start):
+            return P.matmul_mx(pys[b][:, 0:C], T.wcb[:, 128 * b:128 * b + 128], T.wsb[:, 128 * b:128 * b + 128], sc[:], ss[:], start, not start)
+
+        def unpack(b, qc, qs, start, stop):
+            return P.matmul_mx(pys[b][:, 0:C], T.ec[:, 128 * b:128 * b + 128], T.es[:, 128 * b:128 * b + 128], qc[:], qs[:], start, stop)
+
+        layer_first = v > 0 or not O["dfirst"]
+        if v > 0:
+            addresses()
+            compare(O["pre"])
+            wait("P", t_z)
+        if layer_first:
+            wait("P", t_w, *ready)
+            for b in range(4):
+                layer(b, True)
+        need = [t_off, t_m] + ([t_z] if t_z is not None else [])
+        k = O["bcut"]
+        wait("V", *need)
+        t_b1 = inc(V.tensor_copy(T.bt[:, 0:16 * k], T.win[:, 0:wlen].indirect(off[:, 0:k])), "v_b")
+        wait("S", *need)
+        t_b2 = inc(S.activation(T.bt[:, 16 * k:4 * C], T.win[:, 0:wlen].indirect(off[:, k:80]), ACT.Copy), "s_b")
+        if v == 0:
+            wait("V", t_ls)
+            t_neg = inc(ts(T.negb[:], ls[:], -1024.0, OP.mult), "v_neg")
+            addresses()
+        compare(O["mid"] if v > 0 else O["mid0"])
+        wait("V", t_b1)
+        inc(quant(T.bc[:, 0:4 * k], T.bs[:, 0:4 * k], T.bt[:, 0:16 * k]), "q_b")
+        wait("V", t_b2)
+        t_qb = inc(quant(T.bc[:, 4 * k:C], T.bs[:, 4 * k:C], T.bt[:, 16 * k:4 * C]), "q_b")
+        if v == 0:
+            t_nega = inc(ts(T.nega[:], ls[:], -1.0, OP.mult), "v_nega")
+            wait("V", t_k0)
+            for k in range(4):
+                inc(ts(T.k2[:, 64 * k + 1:64 * k + 64], T.i64[:, 1:64], T.k0[:, 16 + k:17 + k], OP.is_equal, T.k0[:, 20 + k:21 + k], OP.mult), "vc")
+            kc["k2"] = inc(ts(T.k2[:, 0:256:64], T.i64[:, 0:4], 0.0, OP.mult, 1048576.0, OP.add), "vc")
+        else:
+            scans((4, 3))
+        wait("P", t_qe, t_qb)
+        t_d = {}
+        if layer_first:
+            for b in (0, 2, 1, 3):
+                t_d[b] = inc(unpack(b, T.bc, T.bs, False, True), "m_d%d" % b)
+        else:
+            for b in range(4):
+                unpack(b, T.bc, T.bs, True, False)
+            wait("P", t_w, *ready)
+            for b in (0, 2, 1, 3):
+                t_d[b] = inc(layer(b, False), "m_d%d" % b)
+        for b in (0, 1):
+            wait("V", t_d[b])
+            t_y1 = inc(ts(T.yt[:, b:4 * C:4], pys[b][:, 0:C], 0.015625, OP.mult), "v_y")
+        for b in (2, 3):
+            wait("S", t_d[b])
+            t_y2 = inc(S.activation(T.yt[:, b:4 * C:4], pys[b][:, 0:C], ACT.Copy, scale=0.015625), "s_y")
+        compare([b for b in (4, 3, 2, 1, 0) if b not in t_cmp])
+        kc["cmp"] = t_cmp[0]
+        wait("V", t_y1, t_y2)
+        if last:
+            t_qy = [inc(quant(oc_[:], os_[:], T.yt[:]), "q_y0")]
+        else:
+            t_qy = quant_halves(oc_, os_, T.yt)
+        dst = home if last else nxt
+        order = O["ret"] if last else O["on"] if topo.chip(dst) == topo.chip(core) else O["off"]
+
+        def send_state(parts):
+            for x in parts:
+                if x == "c":
+                    send(dst, lands[v][0].bitcast(dt.uint8), oc_[:].bitcast(dt.uint8), "ac%d" % (v + 1))
+                else:
+                    send(dst, lands[v][1], os_[:], "as%d" % (v + 1))
+
+        wait("G", *t_qy)
+        send_state(order.split("l")[0])
+        if not last:
+            tba = bits_of(oc_, os_, t_qy)
+            tbb = second_bits()
+            t_w16 = list_products(tba, tbb)
+            scans([b for b in (4, 3, 2, 1, 0) if b not in scanned][:2])
+            wait("V", t_w16)
+            t_lo = inc(V.tensor_copy(sent_lists[v][:], T.pw[:, 0:80:4]), "v_ls")
+            wait("G", t_lo)
+            send(dst, lists[v + 1][:], sent_lists[v][:], "al%d" % (v + 1))
+        send_state(order.split("l")[1])
+        wait("P", *t_qy)
+        t_dy = {}
+        for b in range(4):
+            t_dy[b] = inc(unpack(b, oc_, os_, True, True), "m_d%d" % b)
+        z0 = 4 * (M + v * C)
+        for b in range(4):
+            wait("S", t_dy[b])
+            t_z = inc(S.activation(T.win[:, z0 + b:z0 + 4 * C:4], pys[b][:, 0:C], ACT.Copy, scale=0.015625), "s_z")
+        if v == 0:
+            kc["val"] = inc(S.activation(T.iota[:, M + C:M + 3 * C], T.iota[:, M - C:M + C], ACT.Identity, bias=float(2 * C)), "s_val")
+        scans([b for b in (4, 3, 2, 1, 0) if b not in scanned])
+        wait("V", kc["scan"], t_nega)
+        t = inc(V.tensor_tensor(T.mn[:], T.scn[:, 63:4 * C:64], T.nega[:], OP.min), "v_s")
+        wait("V", t)
+        t = inc(ts(T.sco[:], T.mn[:], -1.0, OP.mult), "v_s")
+        wait("V", t_iota, t_p0 if v == 0 else kc["val"])
+        for b in (4, 3, 2, 1, 0):
+            wait("V", t)
+            a = M + C * v + 64 * b
+            t = inc(V.tensor_copy(T.ptab[:].indirect(T.sco[:, 4 * b:4 * b + 4]), T.iota[:, a:a + 64]), "v_s")
+        t_tab = t
+
+    t_c3, t_s3 = arrival(away, "ac3"), arrival(away, "as3")
+    early = topo.chip(away) == topo.chip(core)
+    wait("P", t_c3, t_s3)
+    t_my = [inc(P.matmul_mx(bank[:, 0:H], T.wcb[:, 0:128], T.wsb[:, 0:128], T.s3c[:, H * i:H * i + H], T.fs[:, H * i:H * i + H], True, True), "m_a%d" % i)
+            for i, bank in enumerate((T.pa, T.pb))]
+
+    def store_y():
+        toks = []
+        for i, bank in enumerate((T.pa, T.pb)):
+            if early or i == 1:
+                wait("S", t_my[i])
+                toks.append(inc(S.activation(T.yo[:, H * i:H * i + H], bank[:, 0:H], ACT.Copy), "s_yo"))
+            else:
+                wait("V", t_my[i])
+                toks.append(inc(V.tensor_copy(T.yo[:, H * i:H * i + H], bank[:, 0:H]), "v_yo"))
+        wait("S", *(toks[1:] if early else toks))
+        inc(S.dma_start(T.y[:], T.yo[:]), "st_y", 16)
+
+    def store_state():
+        wait("Y", t_c3)
+        inc(Y.dma_start(T.oc[:, 0:4 * C], T.s3c[:].bitcast(dt.uint8)), "st", 16)
+
+    if early:
+        store_y()
+        store_state()
+    cut = O["cut"]
+    parts = ((0, cut), (cut, M))
+    t_o = []
+    wait("V", t_tab, kc["k1"])
+    for i, (a, b) in enumerate(parts):
+        t = inc(V.tensor_tensor_scan(T.fsc[:, a:b], T.k1[:, a:b], T.ptab[:, a:b], 0.0, OP.add, OP.min), "v_g")
+        wait("V", t)
+        t_o.append(inc(ts(T.offm[:, a // 4:b // 4], T.fsc[:, a + 3:b:4], 4.0, OP.mult, T.k0[:, 1:2], OP.add), "v_of%d" % i))
+    wait("S", t_o[0], t_z)
+    t_b2 = inc(S.activation(T.mf[:, 0:4 * cut], T.win[:].indirect(T.offm[:, 0:cut // 4]), ACT.Copy), "s_b")
+    wait("V", t_o[1], t_z)
+    t_b1 = inc(V.tensor_copy(T.mf[:, 4 * cut:4 * M], T.win[:].indirect(T.offm[:, cut // 4:M // 4])), "v_b")
+    t_q = []
+    for i, tb in ((1, t_b1), (0, t_b2)):
+        a, b = parts[i]
+        wait("V", tb)
+        t_q.append(inc(quant(T.fc[:, a:b], T.fs[:, C + a:C + b], T.mf[:, 4 * a:4 * b]), "q_m%d" % i))
+        wait("Y", t_q[-1])
+        inc(Y.dma_start(T.oc[:, 4 * (C + a):4 * (C + b)], T.fc[:, a:b].bitcast(dt.uint8)), "st", 16)
+    if not early:
+        store_state()
+        store_y()
+    wait("Y", t_s3)
+    if early:
+        wait("S", t_s3, *t_q)
+    for k in range(4):
+        q, role = (Y, "st") if k < 2 or not early else (S, "st_y")
+        inc(q.dma_start(T.osc[4 * k:4 * k + 4, :], T.fs[32 * k:32 * k + 4, :]), role, 16)
+
+    for role in list(cnt):
+        if top.get(role, 0) < cnt[role]:
+            wait("G", (role, cnt[role]))

@@ -2,7 +2,7 @@ from concourse.mybir import dt, AluOpType, AxisListType, ActivationFunctionType
 
 C, M, VISITS = 320, 512, 3
 CODES, U8, BF, F32, F16, U16, I32 = "float8_e4m3fn_x4", "uint8", "bfloat16", "float32", "float16", "uint16", "int32"
-O = {"dfirst": True, "pre": (4,), "mid": (3, 2), "mid0": (4, 3), "cut": 320, "bcut": 38, "on": "slc", "off": "slc", "ret": "csl"}
+O = {"pre": (4,), "mid": (3,), "mid0": (4, 3), "cut": 192, "bcut": 36}
 
 
 def _sb(n, d):
@@ -27,15 +27,14 @@ SCRATCH = {
     "bt": _sb(4 * C, BF), "bc": _sb(C, CODES), "bs": _sb(C, U8),
     "yt": _sb(4 * C, BF),
     "o1c": _sb(C, CODES), "o1s": _sb(C, U8), "o2c": _sb(C, CODES), "o2s": _sb(C, U8), "o3c": _sb(C, CODES), "o3s": _sb(C, U8),
-    "s1c": _sb(C, CODES), "s1s": _sb(C, U8), "s2c": _sb(C, CODES), "s2s": _sb(C, U8), "s3c": _sb(C, CODES),
-    "fs": _sb(C + M, U8), "fc": _sb(M, CODES), "mf": _sb(4 * M, BF),
+    "s1c": _sb(C, CODES), "s1s": _sb(C, U8), "s2c": _sb(C, CODES), "s2s": _sb(C, U8),
+    "fs": _sb(C + M, U8), "fc": _sb(C + M, CODES), "mf": _sb(4 * M, BF),
     "rep": _sb(C, F32), "negb": _sb(20, F32), "nega": _sb(20, F32),
     "cmp": _sb(4 * C, BF), "scn": _sb(4 * C, BF), "mn": _sb(20, F32), "sco": _sb(20, U16),
     "fsc": _sb(M, F32), "offm": _sb(128, U16), "yo": _sb(C, F32),
-    "py0": ("psum", [128, 512], F32), "py1": ("psum", [128, 512], F32), "py2": ("psum", [128, 512], F32),
-    "py3": ("psum", [128, 512], F32), "pa": ("psum", [128, 512], F32), "pl": ("psum", [128, 512], F32),
-    "pw": ("psum", [128, 512], F32), "pb": ("psum", [128, 512], F32),
 }
+for _i in range(8):
+    SCRATCH["pb%d" % _i] = ("psum", [128, 512], F32)
 REMOTE = ["ac1", "as1", "al1", "ac2", "as2", "al2", "ac3", "as3", "sent"]
 SEMAPHORES = REMOTE + ["z%d" % i for i in range(100)]
 
@@ -50,6 +49,7 @@ def rank_program(g, core, T, topo):
     V, S, P, Y = g.vector, g.scalar, g.tensor, g.sync
     qname = {"V": V, "S": S, "P": P, "Y": Y, "G": g}
     slot, cnt, seen, top = {}, {}, {}, {}
+    bank = [T["pb%d" % i] for i in range(8)]
 
     def sem(role):
         if role in REMOTE:
@@ -83,8 +83,8 @@ def rank_program(g, core, T, topo):
         g.remote_dma(out, src, sem(role), sem("sent"), pid, rid, topo.mask(core, dst))
         cnt["sent"] = cnt.get("sent", 0) + len(topo.engines(core, dst))
 
-    def arrival(src, role):
-        cnt[role] = len(topo.engines(src, core))
+    def arrival(src, role, writes=1):
+        cnt[role] = writes * len(topo.engines(src, core))
         return (role, cnt[role])
 
     nxt, prv = T.cores[(rank + 1) % n], T.cores[(rank - 1) % n]
@@ -149,53 +149,52 @@ def rank_program(g, core, T, topo):
     wait("S", t_iota)
     t_p0 = inc(S.activation(T.ptab[:, 0:M], T.iota[:, 0:M], ACT.Copy), "s_p0")
 
-    H = C // 2
+    kb = O["bcut"]
+    part = ((0, 4 * kb), (4 * kb, C))
 
-    def quant_halves(sc, ss, tile):
-        return [inc(quant(sc[:, H * i:H * i + H], ss[:, H * i:H * i + H], tile[:, 4 * H * i:4 * H * (i + 1)]), "q_y%d" % i) for i in range(2)]
+    def quant_part(i, sc, ss, tile, role):
+        a, b = part[i]
+        return inc(quant(sc[:, a:b], ss[:, a:b], tile[:, 4 * a:4 * b]), role % i)
 
-    def bits_of(sc, ss, ready):
-        ta = []
-        for i, bank in enumerate((T.pa, T.pb)):
-            wait("P", t_qu, ready[i])
-            ta.append(inc(P.matmul_mx(bank[:, 0:H], T.uc[:], T.us[:], sc[:, H * i:H * i + H], ss[:, H * i:H * i + H], True, True), "m_a%d" % i))
-        for i, bank in enumerate((T.pa, T.pb)):
-            wait("V", ta[i])
-            tb = inc(ts(T.bits[:, H * i:H * i + H], bank[:, 0:H], 0.0, OP.is_gt), "v_bits")
+    def address_product(i, sc, ss, ready):
+        a, b = part[i]
+        wait("P", t_qu, ready[i])
+        return inc(P.matmul_mx(bank[i][:, 0:b - a], T.uc[:], T.us[:], sc[:, a:b], ss[:, a:b], True, True), "m_a%d" % i)
+
+    def quant_bits(tb):
         wait("V", tb)
-        return inc(quant(T.bac[:], T.bas[:], T.bits[:, 0:520]), "q_ba")
-
-    def second_bits():
-        return inc(quant(T.bbc[:], T.bbs[:], T.bits[:, 4:524]), "q_bb")
+        return (inc(quant(T.bac[:], T.bas[:], T.bits[:, 0:520]), "q_ba"), inc(quant(T.bbc[:], T.bbs[:], T.bits[:, 4:524]), "q_bb"))
 
     def list_products(tba, tbb):
         for i, s in enumerate((0, 2, 1, 3)):
             wait("P", t_qpw, tba if s % 2 == 0 else tbb)
             bc, bs = (T.bac, T.bas) if s % 2 == 0 else (T.bbc, T.bbs)
             a, o = 12 - 4 * s, s - s % 2
-            ins = P.matmul_mx(T.pw[:, 0:128], T.pwc[:, a:a + 128], T.pws[:, a:a + 128], bc[:, o:o + 128], bs[:, o:o + 128], i == 0, i == 3)
+            ins = P.matmul_mx(bank[2][:, 0:128], T.pwc[:, a:a + 128], T.pws[:, a:a + 128], bc[:, o:o + 128], bs[:, o:o + 128], i == 0, i == 3)
         return inc(ins, "m_w")
 
     wait("V", t_x)
-    t_s0 = quant_halves(T.s0c, T.s0s, T.xt)
-    tba = bits_of(T.s0c, T.s0s, t_s0)
+    t_s0 = [quant_part(i, T.s0c, T.s0s, T.xt, "q_y%d") for i in range(2)]
+    ta = [address_product(i, T.s0c, T.s0s, t_s0) for i in range(2)]
+    for i, (a, b) in enumerate(part):
+        wait("V", ta[i])
+        tb = inc(ts(T.bits[:, a:b], bank[i][:, 0:b - a], 0.0, OP.is_gt), "v_bits")
+    tba, tbb = quant_bits(tb)
     wait("P", t_pl, tba)
-    t_l80 = inc(P.matmul_mx(T.pl[:, 0:128], T.plc[:], T.pls[:], T.bac[:, 0:128], T.bas[:, 0:128], True, True), "m_l")
-    tbb = second_bits()
+    t_l80 = inc(P.matmul_mx(bank[3][:, 0:128], T.plc[:], T.pls[:], T.bac[:, 0:128], T.bas[:, 0:128], True, True), "m_l")
     wait("V", t_l80)
-    t_off = inc(ts(T.off0[:], T.pl[:, 0:80], 4.0, OP.mult, l4, OP.add), "v_off")
+    t_off = inc(ts(T.off0[:], bank[3][:, 0:80], 4.0, OP.mult, l4, OP.add), "v_off")
     t_w16 = list_products(tba, tbb)
     wait("V", t_e)
     for b in range(4):
         t_qe = inc(quant(T.ec[:, 128 * b:128 * b + 128], T.es[:, 128 * b:128 * b + 128], T.et[:, 3 - b:515 - b]), "q_e")
     wait("V", t_w16)
-    t_ls = inc(V.tensor_copy(T.ls0[:], T.pw[:, 0:80:4]), "v_ls")
+    t_ls = t_lo = inc(V.tensor_copy(T.ls0[:], bank[2][:, 0:80:4]), "v_ls")
 
     state = [(T.s0c, T.s0s, t_s0), (T.s1c, T.s1s, None), (T.s2c, T.s2s, None)]
     outs = [(T.o1c, T.o1s), (T.o2c, T.o2s), (T.o3c, T.o3s)]
-    lands = [(T.s1c[:], T.s1s[:]), (T.s2c[:], T.s2s[:]), (T.s3c[:], T.fs[:, 0:C])]
+    lands = [(T.s1c, T.s1s), (T.s2c, T.s2s), (T.fc, T.fs)]
     lists, sent_lists, offs = [T.ls0, T.ls1, T.ls2], [T.lo1, T.lo2], [T.off0, T.off1, T.off2]
-    pys = [T.py0, T.py1, T.py2, T.py3]
     t_z = t_tab = None
 
     for v in range(VISITS):
@@ -205,7 +204,7 @@ def rank_program(g, core, T, topo):
         oc_, os_ = outs[v]
         wlen = 4 * (M + v * C)
         if v > 0:
-            ready = [arrival(prv, "ac%d" % v), arrival(prv, "as%d" % v)]
+            ready = [arrival(prv, "ac%d" % v, 2 if v == 1 else 1), arrival(prv, "as%d" % v)]
             t_ls = arrival(prv, "al%d" % v)
             wait("V", t_ls, t_tab)
             t = inc(V.tensor_copy(T.gg[:], T.ptab[:, 0:M].indirect(ls[:])), "v_g")
@@ -215,7 +214,7 @@ def rank_program(g, core, T, topo):
             t_nega = inc(ts(T.nega[:], ls[:], -1.0, OP.mult), "v_nega")
             wait("V", t)
             t_off = inc(ts(off[:], T.gs[:, 3:C:4], 4.0, OP.mult, T.k0[:, 1:2], OP.add), "v_off")
-        t_cmp, scanned = {}, []
+        t_cmp = {}
 
         def addresses():
             wait("S", t_ls, t_iota)
@@ -228,165 +227,218 @@ def rank_program(g, core, T, topo):
                 for k in range(4 * b, 4 * b + 4):
                     t_cmp[b] = inc(S.activation(T.cmp[:, 64 * k:64 * k + 64], T.rep[:, 64 * b:64 * b + 64], ACT.Abs, bias=T.negb[:, k:k + 1], scale=1024.0), "s_c%d" % b)
 
-        def scans(blocks):
-            wait("V", kc["k2"])
-            for b in blocks:
-                wait("V", t_cmp[b])
-                scanned.append(b)
-                kc["scan"] = inc(V.tensor_tensor_scan(T.scn[:, 256 * b:256 * b + 256], T.k2[:], T.cmp[:, 256 * b:256 * b + 256], 0.0, OP.add, OP.min), "v_s")
+        def scan(b):
+            wait("V", kc["k2"], t_cmp[b])
+            kc["scan"] = inc(V.tensor_tensor_scan(T.scn[:, 256 * b:256 * b + 256], T.k2[:], T.cmp[:, 256 * b:256 * b + 256], 0.0, OP.add, OP.min), "v_s")
 
-        def layer(b, start):
-            return P.matmul_mx(pys[b][:, 0:C], T.wcb[:, 128 * b:128 * b + 128], T.wsb[:, 128 * b:128 * b + 128], sc[:], ss[:], start, not start)
+        def places(a, e):
+            wait("V", kc["scan"], t_nega)
+            kc["mn"] = inc(V.tensor_tensor(T.mn[:, a:e], T.scn[:, 64 * a + 63:64 * e:64], T.nega[:, a:e], OP.min), "v_mn")
 
-        def unpack(b, qc, qs, start, stop):
-            return P.matmul_mx(pys[b][:, 0:C], T.ec[:, 128 * b:128 * b + 128], T.es[:, 128 * b:128 * b + 128], qc[:], qs[:], start, stop)
+        def offsets(a, e):
+            wait("V", kc["mn"])
+            kc["sco"] = inc(ts(T.sco[:, a:e], T.mn[:, a:e], -1.0, OP.mult), "v_sco")
 
-        layer_first = v > 0 or not O["dfirst"]
+        def scatter(b):
+            wait("V", kc["sco"], t_iota, t_p0 if v == 0 else kc["val"])
+            if b < 4:
+                wait("V", kc["tab"])
+            a = M + C * v + 64 * b
+            kc["tab"] = inc(V.tensor_copy(T.ptab[:].indirect(T.sco[:, 4 * b:4 * b + 4]), T.iota[:, a:a + 64]), "v_tab")
+
+        def layer(i, b, start):
+            a, e = part[i]
+            return P.matmul_mx(bank[4 * i + b][:, 0:e - a], T.wcb[:, 128 * b:128 * b + 128], T.wsb[:, 128 * b:128 * b + 128], sc[:, a:e], ss[:, a:e], start, not start)
+
+        def unpack(out, b, qc, qs, start, stop):
+            return P.matmul_mx(out, T.ec[:, 128 * b:128 * b + 128], T.es[:, 128 * b:128 * b + 128], qc, qs, start, stop)
+
+        def unpack_b(i, b, start):
+            a, e = part[i]
+            return unpack(bank[4 * i + b][:, 0:e - a], b, T.bc[:, a:e], T.bs[:, a:e], start, not start)
+
         if v > 0:
             addresses()
             compare(O["pre"])
-            wait("P", t_z)
-        if layer_first:
-            wait("P", t_w, *ready)
-            for b in range(4):
-                layer(b, True)
+            wait("P", t_z, t_lo, *ready)
+            for i in range(2):
+                for b in range(4):
+                    layer(i, b, True)
         need = [t_off, t_m] + ([t_z] if t_z is not None else [])
-        k = O["bcut"]
         wait("V", *need)
-        t_b1 = inc(V.tensor_copy(T.bt[:, 0:16 * k], T.win[:, 0:wlen].indirect(off[:, 0:k])), "v_b")
+        t_b1 = inc(V.tensor_copy(T.bt[:, 0:16 * kb], T.win[:, 0:wlen].indirect(off[:, 0:kb])), "v_b")
         wait("S", *need)
-        t_b2 = inc(S.activation(T.bt[:, 16 * k:4 * C], T.win[:, 0:wlen].indirect(off[:, k:80]), ACT.Copy), "s_b")
+        t_b2 = inc(S.activation(T.bt[:, 16 * kb:4 * C], T.win[:, 0:wlen].indirect(off[:, kb:80]), ACT.Copy), "s_b")
         if v == 0:
             wait("V", t_ls)
             t_neg = inc(ts(T.negb[:], ls[:], -1024.0, OP.mult), "v_neg")
             addresses()
         compare(O["mid"] if v > 0 else O["mid0"])
-        wait("V", t_b1)
-        inc(quant(T.bc[:, 0:4 * k], T.bs[:, 0:4 * k], T.bt[:, 0:16 * k]), "q_b")
-        wait("V", t_b2)
-        t_qb = inc(quant(T.bc[:, 4 * k:C], T.bs[:, 4 * k:C], T.bt[:, 16 * k:4 * C]), "q_b")
+        t_qb = []
+        for i, tb in enumerate((t_b1, t_b2)):
+            wait("V", tb)
+            t_qb.append(quant_part(i, T.bc, T.bs, T.bt, "q_b%d"))
         if v == 0:
             t_nega = inc(ts(T.nega[:], ls[:], -1.0, OP.mult), "v_nega")
             wait("V", t_k0)
             for k in range(4):
                 inc(ts(T.k2[:, 64 * k + 1:64 * k + 64], T.i64[:, 1:64], T.k0[:, 16 + k:17 + k], OP.is_equal, T.k0[:, 20 + k:21 + k], OP.mult), "vc")
             kc["k2"] = inc(ts(T.k2[:, 0:256:64], T.i64[:, 0:4], 0.0, OP.mult, 1048576.0, OP.add), "vc")
-        else:
-            scans((4, 3))
-        wait("P", t_qe, t_qb)
+        wait("P", t_qe)
         t_d = {}
-        if layer_first:
+        for i in range(2):
+            wait("P", t_qb[i])
+            if v == 0:
+                for b in range(4):
+                    unpack_b(i, b, True)
+                wait("P", t_w, *ready)
             for b in (0, 2, 1, 3):
-                t_d[b] = inc(unpack(b, T.bc, T.bs, False, True), "m_d%d" % b)
-        else:
-            for b in range(4):
-                unpack(b, T.bc, T.bs, True, False)
-            wait("P", t_w, *ready)
-            for b in (0, 2, 1, 3):
-                t_d[b] = inc(layer(b, False), "m_d%d" % b)
-        for b in (0, 1):
-            wait("V", t_d[b])
-            t_y1 = inc(ts(T.yt[:, b:4 * C:4], pys[b][:, 0:C], 0.015625, OP.mult), "v_y")
-        for b in (2, 3):
-            wait("S", t_d[b])
-            t_y2 = inc(S.activation(T.yt[:, b:4 * C:4], pys[b][:, 0:C], ACT.Copy, scale=0.015625), "s_y")
-        compare([b for b in (4, 3, 2, 1, 0) if b not in t_cmp])
-        kc["cmp"] = t_cmp[0]
-        wait("V", t_y1, t_y2)
-        if last:
-            t_qy = [inc(quant(oc_[:], os_[:], T.yt[:]), "q_y0")]
-        else:
-            t_qy = quant_halves(oc_, os_, T.yt)
+                t_d[i, b] = inc(unpack_b(i, b, False) if v > 0 else layer(i, b, False), "m_d%d%d" % (i, b))
+        t_y = {}
+
+        def copy_y(i, b):
+            a, e = part[i]
+            out, src = T.yt[:, 4 * a + b:4 * e:4], bank[4 * i + b][:, 0:e - a]
+            wait("V" if b < 2 else "S", t_d[i, b])
+            if b < 2:
+                t_y[i, 0] = inc(ts(out, src, 0.015625, OP.mult), "v_y%d" % i)
+            else:
+                t_y[i, 1] = inc(S.activation(out, src, ACT.Copy, scale=0.015625), "s_y%d" % i)
+
+        for i in range(2):
+            copy_y(i, 2)
+            copy_y(i, 3)
+        copy_y(0, 0)
+        copy_y(0, 1)
+        if v > 0:
+            copy_y(1, 0)
+        wait("V", t_y[0, 0], t_y[0, 1])
+        t_qy = [quant_part(0, oc_, os_, T.yt, "q_y%d")]
+        if v == 0:
+            copy_y(1, 0)
+        copy_y(1, 1)
+        wait("V", t_y[1, 0], t_y[1, 1])
+        t_qy.append(quant_part(1, oc_, os_, T.yt, "q_y%d"))
         dst = home if last else nxt
-        order = O["ret"] if last else O["on"] if topo.chip(dst) == topo.chip(core) else O["off"]
 
-        def send_state(parts):
-            for x in parts:
-                if x == "c":
-                    send(dst, lands[v][0].bitcast(dt.uint8), oc_[:].bitcast(dt.uint8), "ac%d" % (v + 1))
-                else:
-                    send(dst, lands[v][1], os_[:], "as%d" % (v + 1))
+        def send_codes(a, b):
+            send(dst, lands[v][0][:, a:b].bitcast(dt.uint8), oc_[:, a:b].bitcast(dt.uint8), "ac%d" % (v + 1))
 
+        def send_scales():
+            send(dst, lands[v][1][:, 0:C], os_[:], "as%d" % (v + 1))
+
+        if v == 0:
+            wait("G", t_qy[0])
+            send_codes(*part[0])
         wait("G", *t_qy)
-        send_state(order.split("l")[0])
-        if not last:
-            tba = bits_of(oc_, os_, t_qy)
-            tbb = second_bits()
+        if last:
+            send_codes(0, C)
+        if v > 0:
+            send_scales()
+        if last:
+            compare((2, 1, 0))
+            scan(4)
+            scan(3)
+            places(12, 20)
+            scan(2)
+            offsets(12, 20)
+            scan(1)
+        else:
+            ta = [address_product(i, oc_, os_, t_qy) for i in range(2)]
+            for i, (a, b) in enumerate(part):
+                wait("S", ta[i])
+                tb = inc(S.activation(T.bits[:, a:b], bank[i][:, 0:b - a], ACT.Sign, bias=-2.0 ** -120), "s_bits")
+                compare((2,) if i == 0 else (1, 0))
+            scan(4)
+            scan(3)
+            tba, tbb = quant_bits(tb)
             t_w16 = list_products(tba, tbb)
-            scans([b for b in (4, 3, 2, 1, 0) if b not in scanned][:2])
+            places(12, 20)
+            scan(2)
+            offsets(12, 20)
             wait("V", t_w16)
-            t_lo = inc(V.tensor_copy(sent_lists[v][:], T.pw[:, 0:80:4]), "v_ls")
+            t_lo = inc(ts(sent_lists[v][:], bank[2][:, 0:80:4], 0.5, OP.mult, 255.5, OP.add), "v_ls")
+            scan(1)
             wait("G", t_lo)
             send(dst, lists[v + 1][:], sent_lists[v][:], "al%d" % (v + 1))
-        send_state(order.split("l")[1])
+            if v == 0:
+                send_codes(*part[1])
+                send_scales()
+            else:
+                send_codes(0, C)
+        kc["cmp"] = t_cmp[0]
         wait("P", *t_qy)
         t_dy = {}
         for b in range(4):
-            t_dy[b] = inc(unpack(b, oc_, os_, True, True), "m_d%d" % b)
+            t_dy[b] = inc(unpack(bank[4 + b][:, 0:C], b, oc_[:], os_[:], True, True), "m_d1%d" % b)
         z0 = 4 * (M + v * C)
         for b in range(4):
             wait("S", t_dy[b])
-            t_z = inc(S.activation(T.win[:, z0 + b:z0 + 4 * C:4], pys[b][:, 0:C], ACT.Copy, scale=0.015625), "s_z")
+            t_z = inc(S.activation(T.win[:, z0 + b:z0 + 4 * C:4], bank[4 + b][:, 0:C], ACT.Copy, scale=0.015625), "s_z")
         if v == 0:
             kc["val"] = inc(S.activation(T.iota[:, M + C:M + 3 * C], T.iota[:, M - C:M + C], ACT.Identity, bias=float(2 * C)), "s_val")
-        scans([b for b in (4, 3, 2, 1, 0) if b not in scanned])
-        wait("V", kc["scan"], t_nega)
-        t = inc(V.tensor_tensor(T.mn[:], T.scn[:, 63:4 * C:64], T.nega[:], OP.min), "v_s")
-        wait("V", t)
-        t = inc(ts(T.sco[:], T.mn[:], -1.0, OP.mult), "v_s")
-        wait("V", t_iota, t_p0 if v == 0 else kc["val"])
-        for b in (4, 3, 2, 1, 0):
-            wait("V", t)
-            a = M + C * v + 64 * b
-            t = inc(V.tensor_copy(T.ptab[:].indirect(T.sco[:, 4 * b:4 * b + 4]), T.iota[:, a:a + 64]), "v_s")
-        t_tab = t
+        scatter(4)
+        scan(0)
+        scatter(3)
+        places(0, 12)
+        offsets(0, 12)
+        for b in (2, 1, 0):
+            scatter(b)
+        t_tab = kc["tab"]
 
     t_c3, t_s3 = arrival(away, "ac3"), arrival(away, "as3")
     early = topo.chip(away) == topo.chip(core)
+    H = C // 2
     wait("P", t_c3, t_s3)
-    t_my = [inc(P.matmul_mx(bank[:, 0:H], T.wcb[:, 0:128], T.wsb[:, 0:128], T.s3c[:, H * i:H * i + H], T.fs[:, H * i:H * i + H], True, True), "m_a%d" % i)
-            for i, bank in enumerate((T.pa, T.pb))]
+    t_my = [inc(P.matmul_mx(bank[i][:, 0:H], T.wcb[:, 0:128], T.wsb[:, 0:128], T.fc[:, H * i:H * i + H], T.fs[:, H * i:H * i + H], True, True), "m_a%d" % i)
+            for i in range(2)]
 
     def store_y():
         toks = []
-        for i, bank in enumerate((T.pa, T.pb)):
+        for i in range(2):
             if early or i == 1:
                 wait("S", t_my[i])
-                toks.append(inc(S.activation(T.yo[:, H * i:H * i + H], bank[:, 0:H], ACT.Copy), "s_yo"))
+                toks.append(inc(S.activation(T.yo[:, H * i:H * i + H], bank[i][:, 0:H], ACT.Copy), "s_yo"))
             else:
                 wait("V", t_my[i])
-                toks.append(inc(V.tensor_copy(T.yo[:, H * i:H * i + H], bank[:, 0:H]), "v_yo"))
+                toks.append(inc(V.tensor_copy(T.yo[:, H * i:H * i + H], bank[i][:, 0:H]), "v_yo"))
         wait("S", *(toks[1:] if early else toks))
         inc(S.dma_start(T.y[:], T.yo[:]), "st_y", 16)
 
-    def store_state():
-        wait("Y", t_c3)
-        inc(Y.dma_start(T.oc[:, 0:4 * C], T.s3c[:].bitcast(dt.uint8)), "st", 16)
+    def store_codes(a, b):
+        inc(Y.dma_start(T.oc[:, 4 * a:4 * b], T.fc[:, a:b].bitcast(dt.uint8)), "st", 16)
 
     if early:
         store_y()
-        store_state()
+        wait("Y", t_c3)
+        store_codes(0, C)
     cut = O["cut"]
-    parts = ((0, cut), (cut, M))
-    t_o = []
+    parts = ((cut, M), (0, cut))
+    t_o, t_f = [], []
     wait("V", t_tab, kc["k1"])
     for i, (a, b) in enumerate(parts):
-        t = inc(V.tensor_tensor_scan(T.fsc[:, a:b], T.k1[:, a:b], T.ptab[:, a:b], 0.0, OP.add, OP.min), "v_g")
-        wait("V", t)
+        t_f.append(inc(V.tensor_tensor_scan(T.fsc[:, a:b], T.k1[:, a:b], T.ptab[:, a:b], 0.0, OP.add, OP.min), "v_f%d" % i))
+        wait("V", t_f[i])
         t_o.append(inc(ts(T.offm[:, a // 4:b // 4], T.fsc[:, a + 3:b:4], 4.0, OP.mult, T.k0[:, 1:2], OP.add), "v_of%d" % i))
     wait("S", t_o[0], t_z)
-    t_b2 = inc(S.activation(T.mf[:, 0:4 * cut], T.win[:].indirect(T.offm[:, 0:cut // 4]), ACT.Copy), "s_b")
+    t_b2 = inc(S.activation(T.mf[:, 4 * cut:4 * M], T.win[:].indirect(T.offm[:, cut // 4:M // 4]), ACT.Copy), "s_b")
     wait("V", t_o[1], t_z)
-    t_b1 = inc(V.tensor_copy(T.mf[:, 4 * cut:4 * M], T.win[:].indirect(T.offm[:, cut // 4:M // 4])), "v_b")
+    t_b1 = inc(V.tensor_copy(T.mf[:, 0:4 * cut], T.win[:].indirect(T.offm[:, 0:cut // 4])), "v_b")
     t_q = []
     for i, tb in ((1, t_b1), (0, t_b2)):
         a, b = parts[i]
         wait("V", tb)
-        t_q.append(inc(quant(T.fc[:, a:b], T.fs[:, C + a:C + b], T.mf[:, 4 * a:4 * b]), "q_m%d" % i))
-        wait("Y", t_q[-1])
-        inc(Y.dma_start(T.oc[:, 4 * (C + a):4 * (C + b)], T.fc[:, a:b].bitcast(dt.uint8)), "st", 16)
-    if not early:
-        store_state()
+        t_q.append(inc(quant(T.fc[:, C + a:C + b], T.fs[:, C + a:C + b], T.mf[:, 4 * a:4 * b]), "q_m%d" % i))
+    if early:
+        wait("Y", t_q[0])
+        store_codes(C, C + cut)
+        wait("Y", t_q[1])
+        store_codes(C + cut, C + M)
+    else:
+        wait("Y", *t_q)
+        store_codes(C, C + M)
+        wait("Y", t_c3)
+        store_codes(0, C)
         store_y()
     wait("Y", t_s3)
     if early:

@@ -2,7 +2,7 @@ from concourse.mybir import dt, AluOpType, AxisListType, ActivationFunctionType
 
 C, M, VISITS = 320, 512, 3
 CODES, U8, BF, F32, F16, U16, I32 = "float8_e4m3fn_x4", "uint8", "bfloat16", "float32", "float16", "uint16", "int32"
-O = {"pre": (4,), "mid": (3,), "mid0": (4, 3), "cut": 192, "bcut": 36}
+O = {"cut": 192, "bcut": 36}
 
 
 def _sb(n, d):
@@ -203,18 +203,7 @@ def rank_program(g, core, T, topo):
         ls, off = lists[v], offs[v]
         oc_, os_ = outs[v]
         wlen = 4 * (M + v * C)
-        if v > 0:
-            ready = [arrival(prv, "ac%d" % v, 2 if v == 1 else 1), arrival(prv, "as%d" % v)]
-            t_ls = arrival(prv, "al%d" % v)
-            wait("V", t_ls, t_tab)
-            t = inc(V.tensor_copy(T.gg[:], T.ptab[:, 0:M].indirect(ls[:])), "v_g")
-            t_neg = inc(ts(T.negb[:], ls[:], -1024.0, OP.mult), "v_neg")
-            wait("V", t, kc["k1"])
-            t = inc(V.tensor_tensor_scan(T.gs[:], T.k1[:, 0:C], T.gg[:], 0.0, OP.add, OP.min), "v_g")
-            t_nega = inc(ts(T.nega[:], ls[:], -1.0, OP.mult), "v_nega")
-            wait("V", t)
-            t_off = inc(ts(off[:], T.gs[:, 3:C:4], 4.0, OP.mult, T.k0[:, 1:2], OP.add), "v_off")
-        t_cmp = {}
+        t_cmp, t_scan, t_mn, t_sco = {}, {}, {}, {}
 
         def addresses():
             wait("S", t_ls, t_iota)
@@ -229,18 +218,22 @@ def rank_program(g, core, T, topo):
 
         def scan(b):
             wait("V", kc["k2"], t_cmp[b])
-            kc["scan"] = inc(V.tensor_tensor_scan(T.scn[:, 256 * b:256 * b + 256], T.k2[:], T.cmp[:, 256 * b:256 * b + 256], 0.0, OP.add, OP.min), "v_s")
+            t_scan[b] = inc(V.tensor_tensor_scan(T.scn[:, 256 * b:256 * b + 256], T.k2[:], T.cmp[:, 256 * b:256 * b + 256], 0.0, OP.add, OP.min), "v_s%d" % b)
 
-        def places(a, e):
-            wait("V", kc["scan"], t_nega)
-            kc["mn"] = inc(V.tensor_tensor(T.mn[:, a:e], T.scn[:, 64 * a + 63:64 * e:64], T.nega[:, a:e], OP.min), "v_mn")
+        def places(lo, hi):
+            a, e = 4 * lo, 4 * hi + 4
+            wait("V", t_nega, *[t_scan[b] for b in range(lo, hi + 1)])
+            t_mn[lo] = inc(V.tensor_tensor(T.mn[:, a:e], T.scn[:, 64 * a + 63:64 * e:64], T.nega[:, a:e], OP.min), "v_mn%d" % lo)
 
-        def offsets(a, e):
-            wait("V", kc["mn"])
-            kc["sco"] = inc(ts(T.sco[:, a:e], T.mn[:, a:e], -1.0, OP.mult), "v_sco")
+        def offsets(lo, hi):
+            a, e = 4 * lo, 4 * hi + 4
+            wait("V", t_mn[lo])
+            t = inc(ts(T.sco[:, a:e], T.mn[:, a:e], -1.0, OP.mult), "v_sco%d" % lo)
+            for b in range(lo, hi + 1):
+                t_sco[b] = t
 
         def scatter(b):
-            wait("V", kc["sco"], t_iota, t_p0 if v == 0 else kc["val"])
+            wait("V", t_sco[b], t_iota, t_p0 if v == 0 else kc["val"])
             if b < 4:
                 wait("V", kc["tab"])
             a = M + C * v + 64 * b
@@ -258,8 +251,20 @@ def rank_program(g, core, T, topo):
             return unpack(bank[4 * i + b][:, 0:e - a], b, T.bc[:, a:e], T.bs[:, a:e], start, not start)
 
         if v > 0:
+            ready = [arrival(prv, "ac%d" % v, 2 if v == 1 else 1), arrival(prv, "as%d" % v)]
+            t_ls = arrival(prv, "al%d" % v)
+            wait("V", t_ls)
+            t_neg = inc(ts(T.negb[:], ls[:], -1024.0, OP.mult), "v_neg")
             addresses()
-            compare(O["pre"])
+            compare((4, 3))
+            wait("V", t_tab)
+            t = inc(V.tensor_copy(T.gg[:], T.ptab[:, 0:M].indirect(ls[:])), "v_g")
+            t_nega = inc(ts(T.nega[:], ls[:], -1.0, OP.mult), "v_nega")
+            wait("V", t, kc["k1"])
+            t = inc(V.tensor_tensor_scan(T.gs[:], T.k1[:, 0:C], T.gg[:], 0.0, OP.add, OP.min), "v_g")
+            wait("V", t)
+            t_off = inc(ts(off[:], T.gs[:, 3:C:4], 4.0, OP.mult, T.k0[:, 1:2], OP.add), "v_off")
+            scan(4)
             wait("P", t_z, t_lo, *ready)
             for i in range(2):
                 for b in range(4):
@@ -273,7 +278,10 @@ def rank_program(g, core, T, topo):
             wait("V", t_ls)
             t_neg = inc(ts(T.negb[:], ls[:], -1024.0, OP.mult), "v_neg")
             addresses()
-        compare(O["mid"] if v > 0 else O["mid0"])
+            compare((4, 3))
+        else:
+            compare((2,))
+            scan(3)
         t_qb = []
         for i, tb in enumerate((t_b1, t_b2)):
             wait("V", tb)
@@ -312,11 +320,15 @@ def rank_program(g, core, T, topo):
         copy_y(0, 1)
         if v > 0:
             copy_y(1, 0)
+        else:
+            scan(4)
         wait("V", t_y[0, 0], t_y[0, 1])
         t_qy = [quant_part(0, oc_, os_, T.yt, "q_y%d")]
         if v == 0:
+            scan(3)
             copy_y(1, 0)
         copy_y(1, 1)
+        places(3, 4)
         wait("V", t_y[1, 0], t_y[1, 1])
         t_qy.append(quant_part(1, oc_, os_, T.yt, "q_y%d"))
         dst = home if last else nxt
@@ -336,29 +348,24 @@ def rank_program(g, core, T, topo):
         if v > 0:
             send_scales()
         if last:
-            compare((2, 1, 0))
-            scan(4)
-            scan(3)
-            places(12, 20)
-            scan(2)
-            offsets(12, 20)
-            scan(1)
+            compare((1, 0))
         else:
             ta = [address_product(i, oc_, os_, t_qy) for i in range(2)]
             for i, (a, b) in enumerate(part):
                 wait("S", ta[i])
                 tb = inc(S.activation(T.bits[:, a:b], bank[i][:, 0:b - a], ACT.Sign, bias=-2.0 ** -120), "s_bits")
-                compare((2,) if i == 0 else (1, 0))
-            scan(4)
-            scan(3)
+                compare(((2,), (1, 0))[i] if v == 0 else ((1,), (0,))[i])
+        offsets(3, 4)
+        scan(2)
+        scatter(4)
+        if not last:
             tba, tbb = quant_bits(tb)
             t_w16 = list_products(tba, tbb)
-            places(12, 20)
-            scan(2)
-            offsets(12, 20)
+        scan(1)
+        scatter(3)
+        if not last:
             wait("V", t_w16)
             t_lo = inc(ts(sent_lists[v][:], bank[2][:, 0:80:4], 0.5, OP.mult, 255.5, OP.add), "v_ls")
-            scan(1)
             wait("G", t_lo)
             send(dst, lists[v + 1][:], sent_lists[v][:], "al%d" % (v + 1))
             if v == 0:
@@ -377,13 +384,14 @@ def rank_program(g, core, T, topo):
             t_z = inc(S.activation(T.win[:, z0 + b:z0 + 4 * C:4], bank[4 + b][:, 0:C], ACT.Copy, scale=0.015625), "s_z")
         if v == 0:
             kc["val"] = inc(S.activation(T.iota[:, M + C:M + 3 * C], T.iota[:, M - C:M + C], ACT.Identity, bias=float(2 * C)), "s_val")
-        scatter(4)
+        places(1, 2)
         scan(0)
-        scatter(3)
-        places(0, 12)
-        offsets(0, 12)
-        for b in (2, 1, 0):
-            scatter(b)
+        offsets(1, 2)
+        places(0, 0)
+        scatter(2)
+        offsets(0, 0)
+        scatter(1)
+        scatter(0)
         t_tab = kc["tab"]
 
     t_c3, t_s3 = arrival(away, "ac3"), arrival(away, "as3")

@@ -2,7 +2,28 @@ from concourse.mybir import dt, AluOpType, AxisListType, ActivationFunctionType
 
 C, M, VISITS = 320, 512, 3
 CODES, U8, BF, F32, F16, U16, I32 = "float8_e4m3fn_x4", "uint8", "bfloat16", "float32", "float16", "uint16", "int32"
-O = {"cut": 192, "bcut": 36}
+RUN, SEG = 64, 65
+O = {"n0": 160, "pipe": False, "cuts": ((0, 160, 320), (0, 128, 320), (0, 128, 320)), "look": (0, 128, 320),
+     "fin": (0, 128, 320, 512), "fst": (0, 320, 512), "ufirst": ((0, 0), (0, 0), (0, 0)), "batches": ((3, 4), (1, 2), (0, 0)),
+     "split": ((1, 1), (0, 0), (1, 1))}
+
+PLAN = """
+c64 ci1 ci4 ci3 ci0 ci2 k2a cf ca1 ca0 cb4 cb0 cb3 ca3 cb1 ca2 cc1 cb2 pl1 pl3 pl2 pl0 q_u q_pl cm qx1 qx0 et0:S A1.0 pw0:V A0.0 bitz2:S sg1.0 et k11
+sg0.0 k13 pw1 pw3 pw2 k2b pw4 k12 tab0 k10 qa2.0 q_pw qc2.0 L80 q_e1 W02.0 L10.0 q_e2 W12.0 W22.0 of.0 iota2 L00.0 L13.0 q_e0 W32.0 L12.0 L11.0 g1.0:V
+g0.0:S L01.0 lo2.0 q_e3 qb1.0 L02.0 rep.0:S L03.0 qb0.0 k21 U11.0 k23 U13.0 k20 k22 U10.0 own.0 U12.0 y11.0:V y13.0:S U00.0 U02.0 y10.0:V U03.0 y12.0:S
+U01.0 c17.0:V y02.0:S cc slot.0 y01.0:S qy1.0 y03.0:S c13.0:V c6.0:V c7.0:V c16.0:V y00.0:S c14.0:V c4.0:V c5.0:V xd.0 A1.1 c2.0:S k2 qy0.0 c15.0:S
+c11.0:S c19.0:V c12.0:V c18.0:V sg1.1 c8.0:V c9.0:V c10.0:V A0.1 Z0.0 s4.0 sg0.1 Z1.0 s2.0 Z2.0 c3.0:S c1.0:S Z3.0 o4.0 c0.0:S qa2.1 qc2.1 z3.0:S t4.0
+W02.1 W12.1 z1.0:S W22.1 s0.0 W32.1 o2.0 z0.0:S lo2.1 t3.0 z2.0:S o0.0 xl2.0 t2.0 xs.0 t1.0 xc.0 t0.0 xc.1 rep.1:S lk1.1 L11.1 own.1 L12.1 L13.1 sc1.1
+L10.1 c19.1:S c3.1:S c0.1:S of1.1 c9.1:V c16.1:S c14.1:V c5.1:V slot.1 lk0.1 g1.1:S sc0.1 c8.1:V c4.1:V c15.1:V of0.1 c11.1:V c12.1:V c17.1:V c18.1:V
+c13.1:V c7.1:V c2.1:V g0.1:S qb1.1 s4.1 U11.1 c10.1:V c6.1:V U10.1 U13.1 U12.1 y10.1:S qb0.1 L03.1 L02.1 L00.1 y12.1:S c1.1:V y11.1:V U00.1 o4.1 y13.1:V
+U02.1 U03.1 y00.1:S L01.1 y02.1:V U01.1 y03.1:S qy1.1 y01.1:S qy0.1 A1.2 s0.1 sg1.2 t4.1 xs.1 A0.2 Z3.1 s2.1 sg0.2 Z0.1 o0.1 Z1.1 qa2.2 z1.1:S qc2.2
+o2.1 t3.1 W02.2 W12.2 W22.2 W32.2 Z2.1 lo2.2 t2.1 z2.1:S xl2.1 z0.1:S t1.1 xd.1 z3.1:S t0.1 rep.2:S lk1.2 lk0.2 own.2 sc1.2 sc0.2 L03.2 c7.2:S L02.2
+of1.2 c15.2:S c10.2:V c4.2:V L01.2 c16.2:V c12.2:V c17.2:V c2.2:V L00.2 of0.2 c5.2:V c14.2:V c13.2:V g1.2:S c9.2:V c11.2:V c18.2:V c8.2:V slot.2 c19.2:V
+g0.2:V c6.2:S qb0.2 qb1.2 s4.2 U02.2 U03.2 U00.2 y02.2:V U01.2 y03.2:S L13.2 L11.2 y00.2:V y01.2:S U11.2 U13.2 c3.2:V L12.2 o4.2 c0.2:V y11.2:S U12.2
+L10.2 U10.2 y13.2:S qy0.2 y12.2:S t4.2 y10.2:S xc.2 s2.2 c1.2:S t3.2 o2.2 qy1.2 t2.2 Z1.2 xd.2 s0.2 Z3.2 t1.2 z1.2:S Z0.2 xs.2 Z2.2 o0.2 z3.2:S t0.2
+z2.2:S fs2 z0.2:S fo2 fs1 st_c fs0 fg2:S fo1 fo0 fg1:V H1 H0 fg0:S fq2 fq1 st_m1 fq0 h1:S h0:S st_m0 st_s0 st_s3 st_s2 st_y st_s1
+""".split()
+ENG = dict(x.split(":") for x in PLAN if ":" in x)
 
 
 def _sb(n, d):
@@ -17,10 +38,9 @@ SCRATCH = {
     "et": _sb(516, BF), "ec": _sb(512, CODES), "es": _sb(512, U8), "c64": _sb(128, BF),
     "plt": _sb(512, BF), "plc": _sb(128, CODES), "pls": _sb(128, U8),
     "pwt": _sb(560, BF), "pwc": _sb(140, CODES), "pws": _sb(140, U8),
-    "bits": _sb(524, BF), "bac": _sb(130, CODES), "bas": _sb(130, U8), "bbc": _sb(130, CODES), "bbs": _sb(130, U8),
     "qi": _sb(1, I32), "ci": _sb(8, I32), "cf": _sb(8, F32), "i64": _sb(64, F32), "ip4": _sb(128, BF),
     "mm": _sb(16, F32), "wr": _sb(4, F32), "wv": _sb(4, F32), "g4t": _sb(4, F32),
-    "k0": _sb(32, F32), "k1": _sb(512, BF), "k2": _sb(256, BF),
+    "k0": _sb(32, F32), "k1": _sb(512, BF), "k2": _sb(8 * SEG, BF),
     "iota": _sb(M + VISITS * C, F32), "ptab": _sb(768, F32),
     "ls0": _sb(20, U16), "lo1": _sb(20, U16), "lo2": _sb(20, U16), "ls1": _sb(20, U16), "ls2": _sb(20, U16),
     "gg": _sb(C, F16), "gs": _sb(C, F16), "off0": _sb(80, U16), "off1": _sb(80, U16), "off2": _sb(80, U16),
@@ -29,16 +49,76 @@ SCRATCH = {
     "o1c": _sb(C, CODES), "o1s": _sb(C, U8), "o2c": _sb(C, CODES), "o2s": _sb(C, U8), "o3c": _sb(C, CODES), "o3s": _sb(C, U8),
     "s1c": _sb(C, CODES), "s1s": _sb(C, U8), "s2c": _sb(C, CODES), "s2s": _sb(C, U8),
     "fs": _sb(C + M, U8), "fc": _sb(C + M, CODES), "mf": _sb(4 * M, BF),
-    "rep": _sb(C, F32), "negb": _sb(20, F32), "nega": _sb(20, F32),
-    "cmp": _sb(4 * C, BF), "scn": _sb(4 * C, BF), "mn": _sb(20, F32), "sco": _sb(20, U16),
+    "rep": _sb(C, BF), "own": _sb(20, F32),
+    "cmp": _sb(20 * SEG, BF), "scn": _sb(20 * SEG, BF), "sco": _sb(20, U16),
     "fsc": _sb(M, F32), "offm": _sb(128, U16), "yo": _sb(C, F32),
 }
+for _i in range(3):
+    SCRATCH.update({"bit%d" % _i: _sb(524, BF), "ba%dc" % _i: _sb(130, CODES), "ba%ds" % _i: _sb(130, U8), "bb%dc" % _i: _sb(130, CODES), "bb%ds" % _i: _sb(130, U8)})
 for _i in range(8):
     SCRATCH["pb%d" % _i] = ("psum", [128, 512], F32)
-REMOTE = ["ac1", "as1", "al1", "ac2", "as2", "al2", "ac3", "as3", "sent"]
-SEMAPHORES = REMOTE + ["z%d" % i for i in range(100)]
+REMOTE = [a + str(v) for v in (1, 2, 3) for a in ("al", "am", "ac", "ad", "as")] + ["sent"]
+SEMAPHORES = REMOTE + ["z%d" % i for i in range(110)]
 
 OP, ACT = AluOpType, ActivationFunctionType
+
+
+def emit(g, T, steps, order, landed):
+    qs = {"V": g.vector, "S": g.scalar, "P": g.tensor, "Y": g.sync, "G": g}
+    place = {nm: i for i, nm in enumerate(order)}
+    members = {}
+    for nm in order:
+        if steps[nm][3]:
+            members.setdefault((steps[nm][3], steps[nm][0]), []).append(nm)
+    head = {nm: nm for nm in order}
+    heads = {}
+    for (tag, q), ms in members.items():
+        heads.setdefault(tag, []).append(ms[-1])
+        for x in ms:
+            head[x] = ms[-1]
+    known = {q: set() for q in qs}
+    after, waits, needed, before, done = {}, {}, set(), {}, {q: set() for q in "VSP"}
+    for nm in order:
+        q, deps, _, tag = steps[nm]
+        ds = set()
+        for d in deps:
+            ds |= set(heads[d]) if d in heads else {head.get(d, d)}
+        waits[nm] = []
+        for d in sorted(ds, key=lambda d: (-place.get(d, 1 << 30), d)):
+            if d not in known[q] and not (q == "P" and d in steps and steps[d][0] == "P"):
+                assert d in landed or place[d] < place[nm], (nm, d)
+                waits[nm].append(d)
+                needed.add(d)
+                known[q] |= after.get(d, {d})
+        before[nm] = set(known[q])
+        after[nm] = known[q] | {nm} | (set(members[tag, q]) if tag and head[nm] == nm else set())
+        if q in done and nm[:3] not in ("ld_", "st_"):
+            done[q] |= after[nm]
+            after[nm] = set(done[q])
+    token, last, count, stores = dict(landed), {}, {}, []
+    for nm in order:
+        q, _, call, tag = steps[nm]
+        for d in waits[nm]:
+            qs[q].wait_ge(T.sem[token[d][0]], token[d][1])
+        ins = call()
+        h, is_dma = head[nm], nm[:3] in ("ld_", "st_")
+        if ins is None or (h not in needed and not is_dma):
+            continue
+        if h not in token:
+            free = [x for x in last if last[x] in before[nm] and not is_dma]
+            x = free[0] if free else "z%d" % len(count)
+            last.pop(x, None)
+            token[h] = (x, count.setdefault(x, 0))
+        x, k = token[h][0], 16 if is_dma else 1
+        ins.then_inc(T.sem[x], k)
+        count[x] += k
+        token[h] = (x, count[x])
+        if nm == h and not is_dma:
+            last[x] = nm
+        if nm == h and is_dma and h not in needed:
+            stores.append(h)
+    for nm in stores:
+        g.wait_ge(T.sem[token[nm][0]], token[nm][1])
 
 
 def rank_program(g, core, T, topo):
@@ -47,414 +127,292 @@ def rank_program(g, core, T, topo):
         return
     n = len(T.cores)
     V, S, P, Y = g.vector, g.scalar, g.tensor, g.sync
-    qname = {"V": V, "S": S, "P": P, "Y": Y, "G": g}
-    slot, cnt, seen, top = {}, {}, {}, {}
     bank = [T["pb%d" % i] for i in range(8)]
+    steps, order, landed, sent = {}, [], {}, [0]
 
-    def sem(role):
-        if role in REMOTE:
-            return T.sem[role]
-        if role not in slot:
-            slot[role] = "z%d" % len(slot)
-        return T.sem[slot[role]]
+    def now(name, q, deps, call, tag=None):
+        steps[name] = (q, list(deps), call, tag)
+        order.append(name)
 
-    def inc(instr, role, k=1):
-        instr.then_inc(sem(role), k)
-        cnt[role] = cnt.get(role, 0) + k
-        return (role, cnt[role])
-
-    def wait(q, *toks):
-        for role, val in toks:
-            if seen.get((q, role), 0) < val:
-                qname[q].wait_ge(sem(role), val)
-                seen[(q, role)] = val
-                top[role] = max(top.get(role, 0), val)
+    def eng(name, default):
+        return ENG.get(name, default)
 
     def ts(out, in0, s1, op0, s2=None, op1=None):
         if op1 is None:
-            return V.tensor_scalar(out, in0, s1, None, op0)
-        return V.tensor_scalar(out, in0, s1, s2, op0, op1)
+            return lambda: V.tensor_scalar(out, in0, s1, None, op0)
+        return lambda: V.tensor_scalar(out, in0, s1, s2, op0, op1)
 
     def quant(c, s, tile):
-        return V.quantize_mx(c, s, tile)
+        return lambda: V.quantize_mx(c, s, tile)
+
+    def scan(out, keep, data):
+        return lambda: V.tensor_tensor_scan(out, keep, data, 0.0, OP.add, OP.min)
+
+    def act(out, in_, func, **kw):
+        return lambda: S.activation(out, in_, func, **kw)
+
+    def mx(out, wc, ws, xc, xs, start, stop):
+        return lambda: P.matmul_mx(out, wc, ws, xc, xs, start, stop)
+
+    def copy(q, out, in_, scale=None):
+        if q == "S":
+            return act(out, in_, ACT.Copy) if scale is None else act(out, in_, ACT.Copy, scale=scale)
+        return (lambda: V.tensor_copy(out, in_)) if scale is None else ts(out, in_, scale, OP.mult)
 
     def send(dst, out, src, role):
-        rid, pid, _ = topo.addr(dst)
-        g.remote_dma(out, src, sem(role), sem("sent"), pid, rid, topo.mask(core, dst))
-        cnt["sent"] = cnt.get("sent", 0) + len(topo.engines(core, dst))
+        def call():
+            rid, pid, _ = topo.addr(dst)
+            g.remote_dma(out, src, T.sem[role], T.sem["sent"], pid, rid, topo.mask(core, dst))
+            sent[0] += len(topo.engines(core, dst))
+        return call
 
-    def arrival(src, role, writes=1):
-        cnt[role] = writes * len(topo.engines(src, core))
-        return (role, cnt[role])
+    def arrival(src, role):
+        landed[role] = (role, len(topo.engines(src, core)))
+        return role
 
     nxt, prv = T.cores[(rank + 1) % n], T.cores[(rank - 1) % n]
     home, away = T.cores[(rank - (VISITS - 1)) % n], T.cores[(rank + VISITS - 1) % n]
+    n0 = O["n0"]
+    part = ((0, n0), (n0, C))
 
-    t_u = inc(S.dma_start(T.ut[:], T.u[:]), "ld_u", 16)
-    t_x = inc(Y.dma_start(T.xt[:], T.x[:]), "ld_x", 16)
-    t_m = inc(Y.dma_start(T.win[:, 0:4 * M], T.m[:]), "ld_m", 16)
-    inc(Y.dma_start(T.wcb[:].bitcast(dt.uint8), T.wc[:]), "ld_w", 16)
-    t_w = inc(Y.dma_start(T.wsb[:], T.ws[:]), "ld_w", 16)
+    def split(src, dst, v):
+        return O["split"][v][int(topo.chip(src) != topo.chip(dst))]
 
-    t_qi = inc(g.iota(T.qi[:], [[0, 1]], 0, 1), "g_qi")
-    t_i64 = inc(g.iota(T.i64[:], [[1, 64]], 0, 0, allow_small_or_imprecise_dtypes=True), "g_i64")
-    t_ip4 = inc(g.iota(T.ip4[:], [[1, 32], [0, 4]], 0, 0, allow_small_or_imprecise_dtypes=True), "g_ip4")
-    inc(V.memset(T.c64[:], 64.0), "v_e0")
-    t_e0 = inc(V.memset(T.et[:], 0.0), "v_e0")
-    inc(V.memset(T.pwt[:], 0.0), "vc")
-    inc(V.memset(T.bits[:, C:524], 0.0), "vc")
-    wait("G", t_e0)
-    t_e = inc(g.affine_select(T.et[:, 3:515:4], T.c64[:], [[-1, 128]], OP.is_equal, 0.0, 0, 1), "g_e")
-    t_iota = inc(g.iota(T.iota[:, 0:M + C], [[1, M + C]], 0, 0, allow_small_or_imprecise_dtypes=True), "g_iota")
+    now("ld_u", "S", [], lambda: S.dma_start(T.ut[:], T.u[:]))
+    now("ld_x", "Y", [], lambda: Y.dma_start(T.xt[:], T.x[:]))
+    now("ld_m", "Y", [], lambda: Y.dma_start(T.win[:, 0:4 * M], T.m[:]))
+    now("ld_wc", "Y", [], lambda: Y.dma_start(T.wcb[:].bitcast(dt.uint8), T.wc[:]), "w")
+    now("ld_ws", "Y", [], lambda: Y.dma_start(T.wsb[:], T.ws[:]), "w")
 
-    wait("V", t_qi)
-    inc(ts(T.ci[:, 0:1], T.qi[:], 15, OP.bitwise_and), "vc")
-    inc(ts(T.ci[:, 1:2], T.qi[:], 3, OP.bitwise_and), "vc")
-    inc(ts(T.ci[:, 2:3], T.qi[:], 2, OP.logical_shift_right, 3, OP.bitwise_and), "vc")
-    inc(ts(T.ci[:, 3:4], T.qi[:], 4, OP.logical_shift_right), "vc")
-    t = inc(ts(T.ci[:, 4:5], T.qi[:], 2, OP.logical_shift_right, 28, OP.bitwise_and), "vc")
-    wait("V", t)
-    t = inc(V.tensor_copy(T.cf[:, 0:5], T.ci[:, 0:5]), "vc")
+    def iota(out, pattern, base, mult):
+        return lambda: g.iota(out, pattern, base, mult, allow_small_or_imprecise_dtypes=True)
+
+    now("qi", "G", [], lambda: g.iota(T.qi[:], [[0, 1]], 0, 1))
+    now("i64", "G", [], iota(T.i64[:], [[1, 64]], 0, 0))
+    now("ip4", "G", [], iota(T.ip4[:], [[1, 32], [0, 4]], 0, 0))
+    now("iota", "G", [], iota(T.iota[:, 0:M + C], [[1, M + C]], 0, 0))
+    head = len(order)
+    now("c64", "V", [], lambda: V.memset(T.c64[:], 64.0))
+
+    def zeros(name, out, width):
+        if eng(name, "S") == "S":
+            now(name, "S", ["iota"], act(out, T.iota[:, 0:width], ACT.Copy, scale=0.0))
+        else:
+            now(name, "V", [], lambda: V.memset(out, 0.0))
+
+    zeros("et0", T.et[:], 516)
+    zeros("pw0", T.pwt[:], 560)
+    zeros("bitz2", T.bit2[:, C:524], 524 - C)
+    now("et", "G", ["c64", "et0"], lambda: g.affine_select(T.et[:, 3:515:4], T.c64[:], [[-1, 128]], OP.is_equal, 0.0, 0, 1))
+    now("iota2", "G", [], iota(T.iota[:, M + C:M + 3 * C], [[1, 2 * C]], M + C, 0))
+    now("tab0", "G", [], iota(T.ptab[:, 0:M], [[1, M]], 0, 0))
+
+    now("ci0", "V", ["qi"], ts(T.ci[:, 0:1], T.qi[:], 15, OP.bitwise_and), "ci")
+    now("ci1", "V", ["qi"], ts(T.ci[:, 1:2], T.qi[:], 3, OP.bitwise_and), "ci")
+    now("ci2", "V", ["qi"], ts(T.ci[:, 2:3], T.qi[:], 2, OP.logical_shift_right, 3, OP.bitwise_and), "ci")
+    now("ci3", "V", ["qi"], ts(T.ci[:, 3:4], T.qi[:], 4, OP.logical_shift_right), "ci")
+    now("ci4", "V", ["qi"], ts(T.ci[:, 4:5], T.qi[:], 2, OP.logical_shift_right, 28, OP.bitwise_and), "ci")
+    now("cf", "V", ["ci"], lambda: V.tensor_copy(T.cf[:, 0:5], T.ci[:, 0:5]))
     lane, l4, sel, grp, grp4 = [T.cf[:, i:i + 1] for i in range(5)]
-    wait("V", t, t_i64)
-    inc(ts(T.mm[:, 0:9], T.i64[:, 0:9], lane, OP.is_lt, 1.0, OP.add), "vc")
-    inc(ts(T.k0[:, 2:3], sel, 1.0, OP.add), "vc")
-    t = inc(ts(T.g4t[:], T.i64[:, 0:4], grp4, OP.add), "vc")
-    wait("V", t)
-    inc(ts(T.k0[:, 4:8], T.i64[:, 0:4], sel, OP.is_equal, 4096.0, OP.mult), "vc")
-    inc(ts(T.k0[:, 8:12], T.i64[:, 0:4], T.k0[:, 2:3], OP.is_equal, -2048.0, OP.mult), "vc")
-    t = inc(V.tensor_reduce(T.wr[:, 0:1], T.mm[:, 0:9], AxisListType.X, OP.mult), "vc")
-    wait("V", t)
-    t_cm = inc(V.tensor_tensor(T.k0[:, 12:16], T.k0[:, 4:8], T.k0[:, 8:12], OP.add), "v_cm")
-    t = inc(ts(T.wv[:, 0:1], lane, 9.0, OP.is_lt, T.wr[:, 0:1], OP.mult), "vc")
     wgt = T.wv[:, 0:1]
-    wait("V", t, t_ip4)
+    now("ca0", "V", ["cf", "i64"], ts(T.mm[:, 0:9], T.i64[:, 0:9], lane, OP.is_lt, 1.0, OP.add))
+    now("ca3", "V", ["cf", "i64"], ts(T.g4t[:], T.i64[:, 0:4], grp4, OP.add))
+    now("cb4", "V", ["ca0"], lambda: V.tensor_reduce(T.wr[:, 0:1], T.mm[:, 0:9], AxisListType.X, OP.mult))
+    now("cc1", "V", ["cb4"], ts(wgt, lane, 9.0, OP.is_lt, T.wr[:, 0:1], OP.mult))
     for k in range(4):
-        inc(ts(T.plt[:, k:512:4], T.ip4[:], T.g4t[:, k:k + 1], OP.is_equal, wgt, OP.mult), "vc")
+        now("pl%d" % k, "V", ["cc1", "ca3", "ip4"], ts(T.plt[:, k:512:4], T.ip4[:], T.g4t[:, k:k + 1], OP.is_equal, wgt, OP.mult), "pl")
     for k in range(4):
-        inc(ts(T.pwt[:, 48 + 5 * k:560:64], T.i64[:, 0:8], grp, OP.is_equal, wgt, OP.mult), "vc")
-    inc(ts(T.k0[:, 0:1], sel, 3.0, OP.is_lt, 8192.0, OP.mult), "vc")
-    t = inc(ts(T.k0[:, 16:20], T.i64[:, 0:4], 16.0, OP.mult, lane, OP.add), "vc")
-    wait("V", t_u)
-    t_qu = inc(quant(T.uc[:], T.us[:], T.ut[:]), "q_u")
-    wait("V", t)
-    t_pl = inc(quant(T.plc[:], T.pls[:], T.plt[:]), "q_pl")
-    t_qpw = inc(quant(T.pwc[:], T.pws[:], T.pwt[:]), "q_pw")
-    inc(ts(T.k0[:, 1:2], T.k0[:, 0:1], l4, OP.add), "vc")
-    t_k0 = inc(ts(T.k0[:, 20:24], T.k0[:, 16:20], -4.0, OP.mult, -512.0, OP.add), "vc")
-    kc = {}
-    wait("S", t_cm, t_ip4)
+        now("pw%d" % (k + 1), "V", ["cc1", "pw0"], ts(T.pwt[:, 48 + 5 * k:560:64], T.i64[:, 0:8], grp, OP.is_equal, wgt, OP.mult), "pw")
+    now("q_u", "V", ["ld_u"], quant(T.uc[:], T.us[:], T.ut[:]))
+    now("q_pl", "V", ["pl"], quant(T.plc[:], T.pls[:], T.plt[:]))
+    now("q_pw", "V", ["pw"], quant(T.pwc[:], T.pws[:], T.pwt[:]))
+    now("ca1", "V", ["cf"], ts(T.k0[:, 2:3], sel, 1.0, OP.add))
+    now("cb0", "V", ["cf", "i64"], ts(T.k0[:, 4:8], T.i64[:, 0:4], sel, OP.is_equal, 4096.0, OP.mult))
+    now("cb1", "V", ["ca1", "i64"], ts(T.k0[:, 8:12], T.i64[:, 0:4], T.k0[:, 2:3], OP.is_equal, -2048.0, OP.mult))
+    now("cm", "V", ["cb0", "cb1"], lambda: V.tensor_tensor(T.k0[:, 12:16], T.k0[:, 4:8], T.k0[:, 8:12], OP.add))
+    now("cb3", "V", ["cf"], ts(T.k0[:, 0:1], sel, 3.0, OP.is_lt, 8192.0, OP.mult))
+    now("cc", "V", ["cb3"], ts(T.k0[:, 1:2], T.k0[:, 0:1], l4, OP.add))
     for k in range(4):
-        kc["k1"] = inc(S.activation(T.k1[:, k:M:4], T.ip4[:], ACT.Identity, bias=T.k0[:, 12 + k:13 + k], scale=0.0), "s_k1")
-    wait("S", t_iota)
-    t_p0 = inc(S.activation(T.ptab[:, 0:M], T.iota[:, 0:M], ACT.Copy), "s_p0")
+        now("k1%d" % k, "S", ["cm", "ip4"], act(T.k1[:, k:M:4], T.ip4[:], ACT.Identity, bias=T.k0[:, 12 + k:13 + k], scale=0.0), "k1")
+    now("ca2", "V", ["cf", "i64"], ts(T.k0[:, 16:20], T.i64[:, 0:4], 16.0, OP.mult, lane, OP.add))
+    now("cb2", "S", ["ca2"], act(T.k0[:, 20:24], T.k0[:, 16:20], ACT.Identity, bias=-0.5, scale=-1.0 / 256))
+    now("k2a", "S", ["i64"], act(T.k2[:, 0:4 * SEG:SEG], T.i64[:, 0:4], ACT.Identity, bias=2.0, scale=0.0), "k2s")
+    now("k2b", "S", ["i64"], act(T.k2[:, RUN:4 * SEG:SEG], T.i64[:, 0:4], ACT.Identity, bias=0.25, scale=0.0), "k2s")
+    for k in range(4):
+        now("k2%d" % k, "V", ["cb2"], ts(T.k2[:, SEG * k + 1:SEG * k + RUN], T.i64[:, 1:RUN], T.k0[:, 16 + k:17 + k], OP.is_equal, T.k0[:, 20 + k:21 + k], OP.mult), "k2h")
+    now("k2", "S", ["k2h", "k2s"], act(T.k2[:, 4 * SEG:8 * SEG], T.k2[:, 0:4 * SEG], ACT.Copy))
+    if O["pipe"]:
+        for h, (a, b) in enumerate(part):
+            now("bitz%d" % h, "S", ["iota"], act(T["bit%d" % h][:, b - a:524], T.iota[:, b - a:524], ACT.Copy, scale=0.0))
 
-    kb = O["bcut"]
-    part = ((0, 4 * kb), (4 * kb, C))
+    def pieces(v):
+        return [(0, 0, n0, [0]), (1, n0, C, [1])] if v and O["pipe"] else [(2, 0, C, [0, 1])]
 
-    def quant_part(i, sc, ss, tile, role):
-        a, b = part[i]
-        return inc(quant(sc[:, a:b], ss[:, a:b], tile[:, 4 * a:4 * b]), role % i)
+    def addresses(v, sc, ss, ready):
+        out = [T.ls0, T.lo1, T.lo2][v]
+        for h, a0, b0, parts in pieces(v):
+            bits, nm = T["bit%d" % h], (lambda x, d=0, h=h: "%s%d.%d" % (x, h, v + d))
+            old = v > 0 and nm("qa", -1) in steps
+            e = eng("sg%d.%d" % (parts[0], v), "S" if v else "V")
+            for i in parts:
+                a, b = part[i]
+                now("A%d.%d" % (i, v), "P", ["q_u", ready[i]] + (["y0%d.%d" % (i, v - 1)] if v else []),
+                    mx(bank[i][:, 0:b - a], T.uc[:], T.us[:], sc[:, a:b], ss[:, a:b], True, True))
+                deps = ["A%d.%d" % (i, v)] + ([nm("qa", -1), nm("qc", -1)] if old else [])
+                if e == "S":
+                    now("sg%d.%d" % (i, v), "S", deps, act(bits[:, a - a0:b - a0], bank[i][:, 0:b - a], ACT.Sign, bias=-2.0 ** -120))
+                else:
+                    now("sg%d.%d" % (i, v), "V", deps, ts(bits[:, a - a0:b - a0], bank[i][:, 0:b - a], 0.0, OP.is_gt))
+            deps = ["sg%d.%d" % (i, v) for i in parts] + ["bitz%d" % h] + ([nm("W3", -1)] if old else [])
+            now(nm("qa"), "V", deps, quant(T["ba%dc" % h][:], T["ba%ds" % h][:], bits[:, 0:520]))
+            now(nm("qc"), "V", deps, quant(T["bb%dc" % h][:], T["bb%ds" % h][:], bits[:, 4:524]))
+            pb = 2 + h % 2
+            for i, s in enumerate((0, 2, 1, 3)):
+                bc, bs = T["b%s%dc" % ("ab"[s % 2], h)], T["b%s%ds" % ("ab"[s % 2], h)]
+                a, o = 12 - 4 * s, s - s % 2
+                deps = ["q_pw", nm("qa" if s % 2 == 0 else "qc")] + (["y0%d.%d" % (pb, v - 1)] if v else [])
+                now(nm("W%d" % i), "P", deps, mx(bank[pb][:, 0:128], T.pwc[:, a:a + 128], T.pws[:, a:a + 128], bc[:, o:o + 128], bs[:, o:o + 128], i == 0, i == 3))
+            src = bank[pb][:, 0:(b0 - a0) // 4:4]
+            dst_ = out[:, a0 // 16:b0 // 16]
+            now(nm("lo"), "V", [nm("W3")], ts(dst_, src, 0.5, OP.mult, 255.5, OP.add) if e == "S" else copy("V", dst_, src))
 
-    def address_product(i, sc, ss, ready):
-        a, b = part[i]
-        wait("P", t_qu, ready[i])
-        return inc(P.matmul_mx(bank[i][:, 0:b - a], T.uc[:], T.us[:], sc[:, a:b], ss[:, a:b], True, True), "m_a%d" % i)
-
-    def quant_bits(tb):
-        wait("V", tb)
-        return (inc(quant(T.bac[:], T.bas[:], T.bits[:, 0:520]), "q_ba"), inc(quant(T.bbc[:], T.bbs[:], T.bits[:, 4:524]), "q_bb"))
-
-    def list_products(tba, tbb):
-        for i, s in enumerate((0, 2, 1, 3)):
-            wait("P", t_qpw, tba if s % 2 == 0 else tbb)
-            bc, bs = (T.bac, T.bas) if s % 2 == 0 else (T.bbc, T.bbs)
-            a, o = 12 - 4 * s, s - s % 2
-            ins = P.matmul_mx(bank[2][:, 0:128], T.pwc[:, a:a + 128], T.pws[:, a:a + 128], bc[:, o:o + 128], bs[:, o:o + 128], i == 0, i == 3)
-        return inc(ins, "m_w")
-
-    wait("V", t_x)
-    t_s0 = [quant_part(i, T.s0c, T.s0s, T.xt, "q_y%d") for i in range(2)]
-    ta = [address_product(i, T.s0c, T.s0s, t_s0) for i in range(2)]
     for i, (a, b) in enumerate(part):
-        wait("V", ta[i])
-        tb = inc(ts(T.bits[:, a:b], bank[i][:, 0:b - a], 0.0, OP.is_gt), "v_bits")
-    tba, tbb = quant_bits(tb)
-    wait("P", t_pl, tba)
-    t_l80 = inc(P.matmul_mx(bank[3][:, 0:128], T.plc[:], T.pls[:], T.bac[:, 0:128], T.bas[:, 0:128], True, True), "m_l")
-    wait("V", t_l80)
-    t_off = inc(ts(T.off0[:], bank[3][:, 0:80], 4.0, OP.mult, l4, OP.add), "v_off")
-    t_w16 = list_products(tba, tbb)
-    wait("V", t_e)
+        now("qx%d" % i, "V", ["ld_x"], quant(T.s0c[:, a:b], T.s0s[:, a:b], T.xt[:, 4 * a:4 * b]))
+    addresses(0, T.s0c, T.s0s, ["qx0", "qx1"])
+    now("L80", "P", ["q_pl", "qa2.0"], mx(bank[3][:, 0:128], T.plc[:], T.pls[:], T.ba2c[:, 0:128], T.ba2s[:, 0:128], True, True))
+    now("of.0", "V", ["L80", "cf"], ts(T.off0[:], bank[3][:, 0:80], 4.0, OP.mult, l4, OP.add))
     for b in range(4):
-        t_qe = inc(quant(T.ec[:, 128 * b:128 * b + 128], T.es[:, 128 * b:128 * b + 128], T.et[:, 3 - b:515 - b]), "q_e")
-    wait("V", t_w16)
-    t_ls = t_lo = inc(V.tensor_copy(T.ls0[:], bank[2][:, 0:80:4]), "v_ls")
+        now("q_e%d" % b, "V", ["et"], quant(T.ec[:, 128 * b:128 * b + 128], T.es[:, 128 * b:128 * b + 128], T.et[:, 3 - b:515 - b]), "q_e")
 
-    state = [(T.s0c, T.s0s, t_s0), (T.s1c, T.s1s, None), (T.s2c, T.s2s, None)]
+    state = [(T.s0c, T.s0s), (T.s1c, T.s1s), (T.s2c, T.s2s)]
     outs = [(T.o1c, T.o1s), (T.o2c, T.o2s), (T.o3c, T.o3s)]
     lands = [(T.s1c, T.s1s), (T.s2c, T.s2s), (T.fc, T.fs)]
     lists, sent_lists, offs = [T.ls0, T.ls1, T.ls2], [T.lo1, T.lo2], [T.off0, T.off1, T.off2]
-    t_z = t_tab = None
+    batches = O["batches"]
+
+    def meets(a, b, runs):
+        return [j for j in range(len(runs) - 1) if runs[j] < b and runs[j + 1] > a]
 
     for v in range(VISITS):
         last = v == VISITS - 1
-        sc, ss, ready = state[v]
+        sc, ss = state[v]
         ls, off = lists[v], offs[v]
         oc_, os_ = outs[v]
         wlen = 4 * (M + v * C)
-        t_cmp, t_scan, t_mn, t_sco = {}, {}, {}, {}
 
-        def addresses():
-            wait("S", t_ls, t_iota)
-            if v > 0:
-                wait("S", kc["cmp"])
-            wait("S", inc(S.activation(T.rep[:], T.iota[:, 0:M].indirect(ls[:]), ACT.Copy), "s_rep"), t_neg)
+        def N(x, d=0):
+            return "%s.%d" % (x, v + d)
 
-        def compare(blocks):
-            for b in blocks:
-                for k in range(4 * b, 4 * b + 4):
-                    t_cmp[b] = inc(S.activation(T.cmp[:, 64 * k:64 * k + 64], T.rep[:, 64 * b:64 * b + 64], ACT.Abs, bias=T.negb[:, k:k + 1], scale=1024.0), "s_c%d" % b)
-
-        def scan(b):
-            wait("V", kc["k2"], t_cmp[b])
-            t_scan[b] = inc(V.tensor_tensor_scan(T.scn[:, 256 * b:256 * b + 256], T.k2[:], T.cmp[:, 256 * b:256 * b + 256], 0.0, OP.add, OP.min), "v_s%d" % b)
-
-        def places(lo, hi):
-            a, e = 4 * lo, 4 * hi + 4
-            wait("V", t_nega, *[t_scan[b] for b in range(lo, hi + 1)])
-            t_mn[lo] = inc(V.tensor_tensor(T.mn[:, a:e], T.scn[:, 64 * a + 63:64 * e:64], T.nega[:, a:e], OP.min), "v_mn%d" % lo)
-
-        def offsets(lo, hi):
-            a, e = 4 * lo, 4 * hi + 4
-            wait("V", t_mn[lo])
-            t = inc(ts(T.sco[:, a:e], T.mn[:, a:e], -1.0, OP.mult), "v_sco%d" % lo)
-            for b in range(lo, hi + 1):
-                t_sco[b] = t
-
-        def scatter(b):
-            wait("V", t_sco[b], t_iota, t_p0 if v == 0 else kc["val"])
-            if b < 4:
-                wait("V", kc["tab"])
-            a = M + C * v + 64 * b
-            kc["tab"] = inc(V.tensor_copy(T.ptab[:].indirect(T.sco[:, 4 * b:4 * b + 4]), T.iota[:, a:a + 64]), "v_tab")
-
-        def layer(i, b, start):
-            a, e = part[i]
-            return P.matmul_mx(bank[4 * i + b][:, 0:e - a], T.wcb[:, 128 * b:128 * b + 128], T.wsb[:, 128 * b:128 * b + 128], sc[:, a:e], ss[:, a:e], start, not start)
-
-        def unpack(out, b, qc, qs, start, stop):
-            return P.matmul_mx(out, T.ec[:, 128 * b:128 * b + 128], T.es[:, 128 * b:128 * b + 128], qc, qs, start, stop)
-
-        def unpack_b(i, b, start):
-            a, e = part[i]
-            return unpack(bank[4 * i + b][:, 0:e - a], b, T.bc[:, a:e], T.bs[:, a:e], start, not start)
-
-        if v > 0:
-            ready = [arrival(prv, "ac%d" % v, 2 if v == 1 else 1), arrival(prv, "as%d" % v)]
-            t_ls = arrival(prv, "al%d" % v)
-            wait("V", t_ls)
-            t_neg = inc(ts(T.negb[:], ls[:], -1024.0, OP.mult), "v_neg")
-            addresses()
-            compare((4, 3))
-            wait("V", t_tab)
-            t = inc(V.tensor_copy(T.gg[:], T.ptab[:, 0:M].indirect(ls[:])), "v_g")
-            t_nega = inc(ts(T.nega[:], ls[:], -1.0, OP.mult), "v_nega")
-            wait("V", t, kc["k1"])
-            t = inc(V.tensor_tensor_scan(T.gs[:], T.k1[:, 0:C], T.gg[:], 0.0, OP.add, OP.min), "v_g")
-            wait("V", t)
-            t_off = inc(ts(off[:], T.gs[:, 3:C:4], 4.0, OP.mult, T.k0[:, 1:2], OP.add), "v_off")
-            scan(4)
-            wait("P", t_z, t_lo, *ready)
-            for i in range(2):
-                for b in range(4):
-                    layer(i, b, True)
-        need = [t_off, t_m] + ([t_z] if t_z is not None else [])
-        wait("V", *need)
-        t_b1 = inc(V.tensor_copy(T.bt[:, 0:16 * kb], T.win[:, 0:wlen].indirect(off[:, 0:kb])), "v_b")
-        wait("S", *need)
-        t_b2 = inc(S.activation(T.bt[:, 16 * kb:4 * C], T.win[:, 0:wlen].indirect(off[:, kb:80]), ACT.Copy), "s_b")
-        if v == 0:
-            wait("V", t_ls)
-            t_neg = inc(ts(T.negb[:], ls[:], -1024.0, OP.mult), "v_neg")
-            addresses()
-            compare((4, 3))
+        prev = (lambda *x: [N(y, -1) for y in x]) if v else (lambda *x: [])
+        look, cuts = O["look"], O["cuts"][v]
+        looks = [N("lk%d" % j) for j in range(len(look) - 1)] if v else []
+        if v:
+            came = {h: arrival(prv, "a%s%d" % ("lm"[h % 2], v)) for h, _, _, _ in pieces(v)}
+            got = list(came.values())
+            two = split(prv, core, v - 1)
+            ready = [[arrival(prv, "ac%d" % v), arrival(prv, "as%d" % v)], [arrival(prv, ("ad%d" if two else "ac%d") % v), "as%d" % v]]
+            for j in range(len(look) - 1):
+                a, b = look[j], look[j + 1]
+                deps = [came[h] for h, a0, b0, _ in pieces(v) if a0 < b and b0 > a]
+                now(N("lk%d" % j), "V", deps + prev("t0") + (prev("sc%d" % j) if v > 1 else []), copy("V", T.gg[:, a:b], T.ptab[:, 0:M].indirect(ls[:, a // 16:b // 16])))
+                now(N("sc%d" % j), "V", [N("lk%d" % j), "k1"] + (prev("of%d" % j) if v > 1 else []), scan(T.gs[:, a:b], T.k1[:, 0:b - a], T.gg[:, a:b]))
+                now(N("of%d" % j), "V", [N("sc%d" % j), "cc"], ts(off[:, a // 4:b // 4], T.gs[:, a + 3:b:4], 4.0, OP.mult, T.k0[:, 1:2], OP.add))
         else:
-            compare((2,))
-            scan(3)
-        t_qb = []
-        for i, tb in enumerate((t_b1, t_b2)):
-            wait("V", tb)
-            t_qb.append(quant_part(i, T.bc, T.bs, T.bt, "q_b%d"))
-        if v == 0:
-            t_nega = inc(ts(T.nega[:], ls[:], -1.0, OP.mult), "v_nega")
-            wait("V", t_k0)
-            for k in range(4):
-                inc(ts(T.k2[:, 64 * k + 1:64 * k + 64], T.i64[:, 1:64], T.k0[:, 16 + k:17 + k], OP.is_equal, T.k0[:, 20 + k:21 + k], OP.mult), "vc")
-            kc["k2"] = inc(ts(T.k2[:, 0:256:64], T.i64[:, 0:4], 0.0, OP.mult, 1048576.0, OP.add), "vc")
-        wait("P", t_qe)
-        t_d = {}
-        for i in range(2):
-            wait("P", t_qb[i])
-            if v == 0:
-                for b in range(4):
-                    unpack_b(i, b, True)
-                wait("P", t_w, *ready)
-            for b in (0, 2, 1, 3):
-                t_d[i, b] = inc(unpack_b(i, b, False) if v > 0 else layer(i, b, False), "m_d%d%d" % (i, b))
-        t_y = {}
-
-        def copy_y(i, b):
-            a, e = part[i]
-            out, src = T.yt[:, 4 * a + b:4 * e:4], bank[4 * i + b][:, 0:e - a]
-            wait("V" if b < 2 else "S", t_d[i, b])
-            if b < 2:
-                t_y[i, 0] = inc(ts(out, src, 0.015625, OP.mult), "v_y%d" % i)
-            else:
-                t_y[i, 1] = inc(S.activation(out, src, ACT.Copy, scale=0.015625), "s_y%d" % i)
-
-        for i in range(2):
-            copy_y(i, 2)
-            copy_y(i, 3)
-        copy_y(0, 0)
-        copy_y(0, 1)
-        if v > 0:
-            copy_y(1, 0)
-        else:
-            scan(4)
-        wait("V", t_y[0, 0], t_y[0, 1])
-        t_qy = [quant_part(0, oc_, os_, T.yt, "q_y%d")]
-        if v == 0:
-            scan(3)
-            copy_y(1, 0)
-        copy_y(1, 1)
-        places(3, 4)
-        wait("V", t_y[1, 0], t_y[1, 1])
-        t_qy.append(quant_part(1, oc_, os_, T.yt, "q_y%d"))
+            got = ["lo2.0"]
+            ready = [["qx0", "w"], ["qx1", "w"]]
+        zs = prev("z0", "z1", "z2", "z3")
+        for j in range(len(cuts) - 1):
+            a, b = cuts[j], cuts[j + 1]
+            e = eng(N("g%d" % j), "VS"[j % 2])
+            deps = [N("of%d" % k) for k in meets(a, b, look)] if v else ["of.0"]
+            now(N("g%d" % j), e, deps + ["ld_m"] + zs + prev(*["qb%d" % i for i in meets(a, b, (0, n0, C))]),
+                copy(e, T.bt[:, 4 * a:4 * b], T.win[:, 0:wlen].indirect(off[:, a // 4:b // 4])))
+        lists_in = {2 + h % 2: N("lo%d" % h) for h, _, _, _ in pieces(v)}
+        free = [[N("sg0")], [N("sg1")], [lists_in[2]], [lists_in.get(3, "of.0")] + prev("y03")] + [prev("z%d" % b) for b in range(4)]
+        for i, (a, b) in enumerate(part):
+            deps = [N("g%d" % j) for j in meets(a, b, cuts)] + prev(*["U%d%d" % (i, k) for k in range(4)])
+            now(N("qb%d" % i), "V", deps, quant(T.bc[:, a:b], T.bs[:, a:b], T.bt[:, 4 * a:4 * b]))
+            uf = bool(O["ufirst"][v][i])
+            for b4 in range(4):
+                w = slice(128 * b4, 128 * b4 + 128)
+                out = bank[4 * i + b4][:, 0:b - a]
+                un, ln = N("U%d%d" % (i, b4)), N("L%d%d" % (i, b4))
+                now(ln, "P", ready[i] + ([] if uf else free[4 * i + b4]), mx(out, T.wcb[:, w], T.wsb[:, w], sc[:, a:b], ss[:, a:b], not uf, uf))
+                now(un, "P", [N("qb%d" % i), "q_e"] + (free[4 * i + b4] if uf else []), mx(out, T.ec[:, w], T.es[:, w], T.bc[:, a:b], T.bs[:, a:b], uf, not uf))
+                e = eng(N("y%d%d" % (i, b4)), "VVSS"[b4])
+                now(N("y%d%d" % (i, b4)), e, [ln if uf else un] + prev("qy%d" % i), copy(e, T.yt[:, 4 * a + b4:4 * b:4], out, 0.015625))
+            now(N("qy%d" % i), "V", [N("y%d%d" % (i, b4)) for b4 in range(4)], quant(oc_[:, a:b], os_[:, a:b], T.yt[:, 4 * a:4 * b]))
         dst = home if last else nxt
-
-        def send_codes(a, b):
-            send(dst, lands[v][0][:, a:b].bitcast(dt.uint8), oc_[:, a:b].bitcast(dt.uint8), "ac%d" % (v + 1))
-
-        def send_scales():
-            send(dst, lands[v][1][:, 0:C], os_[:], "as%d" % (v + 1))
-
-        if v == 0:
-            wait("G", t_qy[0])
-            send_codes(*part[0])
-        wait("G", *t_qy)
-        if last:
-            send_codes(0, C)
-        if v > 0:
-            send_scales()
-        if last:
-            compare((1, 0))
+        lc, lsc = lands[v]
+        if split(core, dst, v):
+            now(N("xc"), "G", [N("qy0")], send(dst, lc[:, 0:n0].bitcast(dt.uint8), oc_[:, 0:n0].bitcast(dt.uint8), "ac%d" % (v + 1)))
+            now(N("xd"), "G", [N("qy1")], send(dst, lc[:, n0:C].bitcast(dt.uint8), oc_[:, n0:C].bitcast(dt.uint8), "ad%d" % (v + 1)))
         else:
-            ta = [address_product(i, oc_, os_, t_qy) for i in range(2)]
-            for i, (a, b) in enumerate(part):
-                wait("S", ta[i])
-                tb = inc(S.activation(T.bits[:, a:b], bank[i][:, 0:b - a], ACT.Sign, bias=-2.0 ** -120), "s_bits")
-                compare(((2,), (1, 0))[i] if v == 0 else ((1,), (0,))[i])
-        offsets(3, 4)
-        scan(2)
-        scatter(4)
+            now(N("xc"), "G", [], lambda: None)
+            now(N("xd"), "G", [N("qy0"), N("qy1")], send(dst, lc[:, 0:C].bitcast(dt.uint8), oc_[:, 0:C].bitcast(dt.uint8), "ac%d" % (v + 1)))
+        now(N("xs"), "G", [N("qy0"), N("qy1")], send(dst, lsc[:, 0:C], os_[:], "as%d" % (v + 1)))
         if not last:
-            tba, tbb = quant_bits(tb)
-            t_w16 = list_products(tba, tbb)
-        scan(1)
-        scatter(3)
-        if not last:
-            wait("V", t_w16)
-            t_lo = inc(ts(sent_lists[v][:], bank[2][:, 0:80:4], 0.5, OP.mult, 255.5, OP.add), "v_ls")
-            wait("G", t_lo)
-            send(dst, lists[v + 1][:], sent_lists[v][:], "al%d" % (v + 1))
-            if v == 0:
-                send_codes(*part[1])
-                send_scales()
-            else:
-                send_codes(0, C)
-        kc["cmp"] = t_cmp[0]
-        wait("P", *t_qy)
-        t_dy = {}
-        for b in range(4):
-            t_dy[b] = inc(unpack(bank[4 + b][:, 0:C], b, oc_[:], os_[:], True, True), "m_d1%d" % b)
+            addresses(v + 1, oc_, os_, [N("qy0"), N("qy1")])
+            for h, a0, b0, _ in pieces(v + 1):
+                now(N("xl%d" % h), "G", [N("lo%d" % h, 1)], send(dst, lists[v + 1][:, a0 // 16:b0 // 16], sent_lists[v][:, a0 // 16:b0 // 16], "a%s%d" % ("lm"[h % 2], v + 1)))
         z0 = 4 * (M + v * C)
         for b in range(4):
-            wait("S", t_dy[b])
-            t_z = inc(S.activation(T.win[:, z0 + b:z0 + 4 * C:4], bank[4 + b][:, 0:C], ACT.Copy, scale=0.015625), "s_z")
-        if v == 0:
-            kc["val"] = inc(S.activation(T.iota[:, M + C:M + 3 * C], T.iota[:, M - C:M + C], ACT.Identity, bias=float(2 * C)), "s_val")
-        places(1, 2)
-        scan(0)
-        offsets(1, 2)
-        places(0, 0)
-        scatter(2)
-        offsets(0, 0)
-        scatter(1)
-        scatter(0)
-        t_tab = kc["tab"]
+            now(N("Z%d" % b), "P", [N("qy0"), N("qy1"), N("y1%d" % b), "q_e"], mx(bank[4 + b][:, 0:C], T.ec[:, 128 * b:128 * b + 128], T.es[:, 128 * b:128 * b + 128], oc_[:], os_[:], True, True))
+            e = eng(N("z%d" % b), "S")
+            now(N("z%d" % b), e, [N("Z%d" % b)], copy(e, T.win[:, z0 + b:z0 + 4 * C:4], bank[4 + b][:, 0:C], 0.015625))
+        scans = prev(*["s%d" % hi for lo_, hi in batches])
+        compares = prev(*["c%d" % k for k in range(20)])
+        now(N("own"), "V", got + scans + compares, ts(T.own[:], ls[:], -1.0, OP.mult, 256.0, OP.add))
+        now(N("slot"), "V", got + scans, ts(T.cmp[:, RUN:20 * SEG:SEG], ls[:], -1.0 / 1024, OP.mult, 0.25, OP.add))
+        e = eng(N("rep"), "S")
+        now(N("rep"), e, got + ["iota"] + compares,
+            act(T.rep[:], T.iota[:, 0:M].indirect(ls[:]), ACT.Identity, bias=256.0, scale=-1.0) if e == "S" else ts(T.rep[:], T.iota[:, 0:M].indirect(ls[:]), -1.0, OP.mult, 256.0, OP.add))
+        for lo_, hi in batches:
+            for k in range(4 * hi + 3, 4 * lo_ - 1, -1):
+                e = eng(N("c%d" % k), "S")
+                w, r = 16 * (k % 4 + 1) if v else RUN, RUN * (k // 4)
+                out, src = T.cmp[:, SEG * k:SEG * k + w], T.rep[:, r:r + w]
+                now(N("c%d" % k), e, [N("own"), N("rep")] + prev("s%d" % hi),
+                    ts(out, src, T.own[:, k:k + 1], OP.not_equal) if e == "V" else act(out, src, ACT.Abs, bias=T.own[:, k:k + 1], scale=-1.0), N("cmp%d" % hi))
+            a, b = 4 * SEG * lo_, 4 * SEG * (hi + 1)
+            now(N("s%d" % hi), "V", [N("cmp%d" % hi), N("slot"), "k2"] + prev("o%d" % hi), scan(T.scn[:, a:b], T.k2[:, 0:b - a], T.cmp[:, a:b]))
+            now(N("o%d" % hi), "V", [N("s%d" % hi)] + prev("t0"), ts(T.sco[:, 4 * lo_:4 * hi + 4], T.scn[:, a + RUN:b:SEG], -1024.0, OP.mult, 256.0, OP.add))
+            for r in range(hi, lo_ - 1, -1):
+                deps = [N("o%d" % hi), "iota", "iota2", "tab0"] + ([N("t%d" % (r + 1))] if r < 4 else looks)
+                a = M + C * v + RUN * r
+                now(N("t%d" % r), "V", deps, copy("V", T.ptab[:].indirect(T.sco[:, 4 * r:4 * r + 4]), T.iota[:, a:a + RUN]))
 
-    t_c3, t_s3 = arrival(away, "ac3"), arrival(away, "as3")
-    early = topo.chip(away) == topo.chip(core)
-    H = C // 2
-    wait("P", t_c3, t_s3)
-    t_my = [inc(P.matmul_mx(bank[i][:, 0:H], T.wcb[:, 0:128], T.wsb[:, 0:128], T.fc[:, H * i:H * i + H], T.fs[:, H * i:H * i + H], True, True), "m_a%d" % i)
-            for i in range(2)]
+    two = split(away, core, VISITS - 1)
+    back = [[arrival(away, "ac3"), arrival(away, "as3")], [arrival(away, "ad3" if two else "ac3"), "as3"]]
 
-    def store_y():
-        toks = []
-        for i in range(2):
-            if early or i == 1:
-                wait("S", t_my[i])
-                toks.append(inc(S.activation(T.yo[:, H * i:H * i + H], bank[i][:, 0:H], ACT.Copy), "s_yo"))
-            else:
-                wait("V", t_my[i])
-                toks.append(inc(V.tensor_copy(T.yo[:, H * i:H * i + H], bank[i][:, 0:H]), "v_yo"))
-        wait("S", *(toks[1:] if early else toks))
-        inc(S.dma_start(T.y[:], T.yo[:]), "st_y", 16)
+    def store(name, deps, out, src, q):
+        q = eng(name, q)
+        now(name, q, deps, lambda: (S if q == "S" else Y).dma_start(out, src))
 
-    def store_codes(a, b):
-        inc(Y.dma_start(T.oc[:, 4 * a:4 * b], T.fc[:, a:b].bitcast(dt.uint8)), "st", 16)
-
-    if early:
-        store_y()
-        wait("Y", t_c3)
-        store_codes(0, C)
-    cut = O["cut"]
-    parts = ((cut, M), (0, cut))
-    t_o, t_f = [], []
-    wait("V", t_tab, kc["k1"])
-    for i, (a, b) in enumerate(parts):
-        t_f.append(inc(V.tensor_tensor_scan(T.fsc[:, a:b], T.k1[:, a:b], T.ptab[:, a:b], 0.0, OP.add, OP.min), "v_f%d" % i))
-        wait("V", t_f[i])
-        t_o.append(inc(ts(T.offm[:, a // 4:b // 4], T.fsc[:, a + 3:b:4], 4.0, OP.mult, T.k0[:, 1:2], OP.add), "v_of%d" % i))
-    wait("S", t_o[0], t_z)
-    t_b2 = inc(S.activation(T.mf[:, 4 * cut:4 * M], T.win[:].indirect(T.offm[:, cut // 4:M // 4]), ACT.Copy), "s_b")
-    wait("V", t_o[1], t_z)
-    t_b1 = inc(V.tensor_copy(T.mf[:, 0:4 * cut], T.win[:].indirect(T.offm[:, 0:cut // 4])), "v_b")
-    t_q = []
-    for i, tb in ((1, t_b1), (0, t_b2)):
-        a, b = parts[i]
-        wait("V", tb)
-        t_q.append(inc(quant(T.fc[:, C + a:C + b], T.fs[:, C + a:C + b], T.mf[:, 4 * a:4 * b]), "q_m%d" % i))
-    if early:
-        wait("Y", t_q[0])
-        store_codes(C, C + cut)
-        wait("Y", t_q[1])
-        store_codes(C + cut, C + M)
-    else:
-        wait("Y", *t_q)
-        store_codes(C, C + M)
-        wait("Y", t_c3)
-        store_codes(0, C)
-        store_y()
-    wait("Y", t_s3)
-    if early:
-        wait("S", t_s3, *t_q)
+    fin = O["fin"]
+    fst, fq = O.get("fst", fin), O.get("fq", fin)
+    for i in range(len(fin) - 1):
+        a, b = fin[i], fin[i + 1]
+        e = eng("fg%d" % i, "SV"[i % 2])
+        now("fs%d" % i, "V", [N("t0"), "k1"], scan(T.fsc[:, a:b], T.k1[:, a:b], T.ptab[:, a:b]))
+        now("fo%d" % i, "V", ["fs%d" % i, "cc"], ts(T.offm[:, a // 4:b // 4], T.fsc[:, a + 3:b:4], 4.0, OP.mult, T.k0[:, 1:2], OP.add))
+        now("fg%d" % i, e, ["fo%d" % i] + [N("z%d" % b4) for b4 in range(4)], copy(e, T.mf[:, 4 * a:4 * b], T.win[:].indirect(T.offm[:, a // 4:b // 4])))
+    for i in range(len(fq) - 1):
+        a, b = fq[i], fq[i + 1]
+        now("fq%d" % i, "V", ["fg%d" % j for j in meets(a, b, fin)], quant(T.fc[:, C + a:C + b], T.fs[:, C + a:C + b], T.mf[:, 4 * a:4 * b]))
+    for i in range(len(fst) - 1):
+        a, b = fst[i], fst[i + 1]
+        store("st_m%d" % i, ["fq%d" % j for j in meets(a, b, fq)], T.oc[:, 4 * (C + a):4 * (C + b)], T.fc[:, C + a:C + b].bitcast(dt.uint8), "Y")
+    for i, (a, b) in enumerate(part):
+        now("H%d" % i, "P", back[i] + [N("y0%d" % i)], mx(bank[i][:, 0:b - a], T.wcb[:, 0:128], T.wsb[:, 0:128], T.fc[:, a:b], T.fs[:, a:b], True, True))
+        e = eng("h%d" % i, "S")
+        now("h%d" % i, e, ["H%d" % i], copy(e, T.yo[:, a:b], bank[i][:, 0:b - a]))
+    store("st_c", [back[0][0], back[1][0]], T.oc[:, 0:4 * C], T.fc[:, 0:C].bitcast(dt.uint8), "Y")
+    store("st_y", ["h0", "h1"], T.y[:], T.yo[:], "Y")
     for k in range(4):
-        q, role = (Y, "st") if k < 2 or not early else (S, "st_y")
-        inc(q.dma_start(T.osc[4 * k:4 * k + 4, :], T.fs[32 * k:32 * k + 4, :]), role, 16)
+        store("st_s%d" % k, ["as3"] + ["fq%d" % i for i in range(len(fq) - 1)], T.osc[4 * k:4 * k + 4, :], T.fs[32 * k:32 * k + 4, :], "YYSS"[k])
 
-    for role in list(cnt):
-        if top.get(role, 0) < cnt[role]:
-            wait("G", (role, cnt[role]))
+    plan = [x.split(":")[0] for x in PLAN]
+    assert sorted(plan) == sorted(order[head:])
+    emit(g, T, steps, order[:head] + plan, landed)
+    g.wait_ge(T.sem["sent"], sent[0])

@@ -3,25 +3,27 @@ from concourse.mybir import dt, AluOpType, AxisListType, ActivationFunctionType
 C, M, VISITS = 320, 512, 3
 CODES, U8, BF, F32, F16, U16, I32 = "float8_e4m3fn_x4", "uint8", "bfloat16", "float32", "float16", "uint16", "int32"
 RUN, SEG = 64, 65
-O = {"n0": 160, "pipe": False, "cuts": ((0, 160, 320), (0, 128, 320), (0, 128, 320)), "look": (0, 128, 320),
-     "fin": (0, 128, 320, 512), "fst": (0, 320, 512), "ufirst": ((0, 0), (0, 0), (0, 0)), "batches": ((3, 4), (1, 2), (0, 0)),
-     "split": ((1, 1), (0, 0), (1, 1))}
+O = {"n0": 128, "pipe": False, "cuts": ((0, 64, 128, 224, 320),) * 3, "look": (0, 128, 320),
+     "fin": (0, 64, 128, 192, 256, 320, 384, 448, 512), "fq": (0, 128, 256, 384, 512), "fst": (0, 256, 512), "zsplit": 1,
+     "ufirst": ((0, 0), (0, 0), (0, 0)), "batches": ((3, 4), (1, 2), (0, 0)), "split": ((1, 1), (0, 0), (1, 1))}
 
 PLAN = """
-c64 ci1 ci4 ci3 ci0 ci2 k2a cf ca1 ca0 cb4 cb0 cb3 ca3 cb1 ca2 cc1 cb2 pl1 pl3 pl2 pl0 q_u q_pl cm qx1 qx0 et0:S A1.0 pw0:V A0.0 bitz2:S sg1.0 et k11
-sg0.0 k13 pw1 pw3 pw2 k2b pw4 k12 tab0 k10 qa2.0 q_pw qc2.0 L80 q_e1 W02.0 L10.0 q_e2 W12.0 W22.0 of.0 iota2 L00.0 L13.0 q_e0 W32.0 L12.0 L11.0 g1.0:V
-g0.0:S L01.0 lo2.0 q_e3 qb1.0 L02.0 rep.0:S L03.0 qb0.0 k21 U11.0 k23 U13.0 k20 k22 U10.0 own.0 U12.0 y11.0:V y13.0:S U00.0 U02.0 y10.0:V U03.0 y12.0:S
-U01.0 c17.0:V y02.0:S cc slot.0 y01.0:S qy1.0 y03.0:S c13.0:V c6.0:V c7.0:V c16.0:V y00.0:S c14.0:V c4.0:V c5.0:V xd.0 A1.1 c2.0:S k2 qy0.0 c15.0:S
-c11.0:S c19.0:V c12.0:V c18.0:V sg1.1 c8.0:V c9.0:V c10.0:V A0.1 Z0.0 s4.0 sg0.1 Z1.0 s2.0 Z2.0 c3.0:S c1.0:S Z3.0 o4.0 c0.0:S qa2.1 qc2.1 z3.0:S t4.0
-W02.1 W12.1 z1.0:S W22.1 s0.0 W32.1 o2.0 z0.0:S lo2.1 t3.0 z2.0:S o0.0 xl2.0 t2.0 xs.0 t1.0 xc.0 t0.0 xc.1 rep.1:S lk1.1 L11.1 own.1 L12.1 L13.1 sc1.1
-L10.1 c19.1:S c3.1:S c0.1:S of1.1 c9.1:V c16.1:S c14.1:V c5.1:V slot.1 lk0.1 g1.1:S sc0.1 c8.1:V c4.1:V c15.1:V of0.1 c11.1:V c12.1:V c17.1:V c18.1:V
-c13.1:V c7.1:V c2.1:V g0.1:S qb1.1 s4.1 U11.1 c10.1:V c6.1:V U10.1 U13.1 U12.1 y10.1:S qb0.1 L03.1 L02.1 L00.1 y12.1:S c1.1:V y11.1:V U00.1 o4.1 y13.1:V
-U02.1 U03.1 y00.1:S L01.1 y02.1:V U01.1 y03.1:S qy1.1 y01.1:S qy0.1 A1.2 s0.1 sg1.2 t4.1 xs.1 A0.2 Z3.1 s2.1 sg0.2 Z0.1 o0.1 Z1.1 qa2.2 z1.1:S qc2.2
-o2.1 t3.1 W02.2 W12.2 W22.2 W32.2 Z2.1 lo2.2 t2.1 z2.1:S xl2.1 z0.1:S t1.1 xd.1 z3.1:S t0.1 rep.2:S lk1.2 lk0.2 own.2 sc1.2 sc0.2 L03.2 c7.2:S L02.2
-of1.2 c15.2:S c10.2:V c4.2:V L01.2 c16.2:V c12.2:V c17.2:V c2.2:V L00.2 of0.2 c5.2:V c14.2:V c13.2:V g1.2:S c9.2:V c11.2:V c18.2:V c8.2:V slot.2 c19.2:V
-g0.2:V c6.2:S qb0.2 qb1.2 s4.2 U02.2 U03.2 U00.2 y02.2:V U01.2 y03.2:S L13.2 L11.2 y00.2:V y01.2:S U11.2 U13.2 c3.2:V L12.2 o4.2 c0.2:V y11.2:S U12.2
-L10.2 U10.2 y13.2:S qy0.2 y12.2:S t4.2 y10.2:S xc.2 s2.2 c1.2:S t3.2 o2.2 qy1.2 t2.2 Z1.2 xd.2 s0.2 Z3.2 t1.2 z1.2:S Z0.2 xs.2 Z2.2 o0.2 z3.2:S t0.2
-z2.2:S fs2 z0.2:S fo2 fs1 st_c fs0 fg2:S fo1 fo0 fg1:V H1 H0 fg0:S fq2 fq1 st_m1 fq0 h1:S h0:S st_m0 st_s0 st_s3 st_s2 st_y st_s1
+ci0 ci4 ci2 ci1 ci3 k2a cf ca0 ca3 ca1 cb4 ca2 cb1 cb0 c64 cc1 pl1 pl2 pl3 pl0 q_u qx1 qx0 et0:S A1.0 pw0:V A0.0 sg1.0 bitz2:S sg0.0 et pw1 pw4 pw3 cm
+q_pl pw2 L00.0 k11 xc.1 tab0 qa2.0 k13 qc2.0 cb2 k10 q_e3 L80 L13.0 of.0 q_pw q_e1 g3.0:S L03.0 L12.0 iota2 g2.0:V L10.0 W02.0 W12.0 W22.0 W32.0 g0.0:S
+q_e0 cb3 lo2.0 q_e2 g1.0:S qb1.0 L02.0 L11.0 slot.0 k22 k2b own.0 rep.0:S k21 U11.0 qb0.0 U12.0 U10.0 y11.0:V U13.0 y12.0:S U03.0 y10.0:V U00.0 y13.0:S
+U02.0 L01.0 c17.0:V c14.0:V U01.0 c19.0:V y03.0:S k23 k20 c16.0:V y02.0:S qy1.0 y00.0:S y01.0:S c3.0:V c8.0:V c18.0:V c12.0:V c13.0:V k2 c15.0:V c0.0:V
+xd.0 c11.0:V c4.0:V c6.0:V c5.0:S A1.1 qy0.0 c10.0:S c9.0:S s4.0 sg1.1 A0.1 k12 c7.0:V Z2.0 cc c2.0:V Z0.0 sg0.1 o4.0 s2.0 Z1.0 z2.0:S t4.0 c1.0:S
+z0.0:S qa2.1 qc2.1 t3.0 W02.1 W12.1 W22.1 o2.0 s0.0 W32.1 Z3.0 lo2.1 t2.0 z3.0:S xl2.0 o0.0 z1.0:S t1.0 xs.0 t0.0 xc.0 rep.1:S lk1.1 lk0.1 sc1.1 L13.1
+own.1 L10.1 sc0.1 L11.1 of1.1 c7.1:S L12.1 c18.1:V c19.1:V c17.1:S slot.1 c15.1:S of0.1 c9.1:V g3.1:S g2.1:V L02.1 L03.1 g1.1:V g0.1:S c16.1:S qb1.1
+c12.1:S c13.1:S c6.1:S c14.1:V c3.1:S c1.1:V c8.1:V qb0.1 c2.1:S U11.1 c5.1:V s4.1 U13.1 y11.1:S U10.1 U12.1 y13.1:V y10.1:S U02.1 U03.1 y12.1:V L00.1
+y02.1:S U00.1 L01.1 y03.1:V U01.1 y00.1:S y01.1:S qy1.1 c11.1:S c10.1:S c0.1:S o4.1 c4.1:S qy0.1 A1.2 t4.1 sg1.2 xs.1 A0.2 s2.1 Z2.1 sg0.2 Z1.1 z2.1:S
+Z0.1 qa2.2 z1.1:S qc2.2 o2.1 t3.1 W02.2 z0.1:S W12.2 W22.2 s0.1 W32.2 Z3.1 lo2.2 t2.1 z3.1:S xl2.1 o0.1 t1.1 xd.1 t0.1 rep.2:S lk0.2 lk1.2 sc0.2 own.2
+L00.2 of0.2 c7.2:S c4.2:V c9.2:V sc1.2 L02.2 c14.2:S L03.2 c18.2:S c2.2:V g0.2:V g1.2:S of1.2 c17.2:S c15.2:V c13.2:V c19.2:S c12.2:V c5.2:V c16.2:V
+slot.2 c6.2:V qb0.2 g3.2:S g2.2:V U03.2 U02.2 U00.2 y03.2:S L01.2 U01.2 s4.2 y00.2:S L11.2 L13.2 y02.2:S L12.2 qb1.2 y01.2:S L10.2 c1.2:S c8.2:V c0.2:V
+c10.2:S o4.2 c11.2:S c3.2:S U11.2 qy0.2 U13.2 t4.2 U12.2 y11.2:S U10.2 xc.2 s2.2 y12.2:S Z03.2 Z00.2 Z01.2 y13.2:S Z02.2 t3.2 y10.2:S o2.2 s0.2 z01.2:S
+t2.2 z00.2:S z03.2:S qy1.2 z02.2:S t1.2 xs.2 Z13.2 o0.2 Z11.2 z13.2:S Z10.2 t0.2 Z12.2 z11.2:S xd.2 z12.2:S fs6 z10.2:S fs4 fs2 fo6 fs7 fs5 fs1 fs0
+fg6:S fo4 fo2 fs3 fo5 H0 fo1 fo0 fo7 fg2:V fg4:S fo3 fg5:V fg7:S st_c H1 fg3:V fg1:S fq3 fg0:S fq2 fq1 h0:S fq0 st_m1 h1:S st_m0 st_s3 st_s2 st_y st_s1
+st_s0
 """.split()
 ENG = dict(x.split(":") for x in PLAN if ":" in x)
 
@@ -355,11 +357,15 @@ def rank_program(g, core, T, topo):
             addresses(v + 1, oc_, os_, [N("qy0"), N("qy1")])
             for h, a0, b0, _ in pieces(v + 1):
                 now(N("xl%d" % h), "G", [N("lo%d" % h, 1)], send(dst, lists[v + 1][:, a0 // 16:b0 // 16], sent_lists[v][:, a0 // 16:b0 // 16], "a%s%d" % ("lm"[h % 2], v + 1)))
-        z0 = 4 * (M + v * C)
-        for b in range(4):
-            now(N("Z%d" % b), "P", [N("qy0"), N("qy1"), N("y1%d" % b), "q_e"], mx(bank[4 + b][:, 0:C], T.ec[:, 128 * b:128 * b + 128], T.es[:, 128 * b:128 * b + 128], oc_[:], os_[:], True, True))
-            e = eng(N("z%d" % b), "S")
-            now(N("z%d" % b), e, [N("Z%d" % b)], copy(e, T.win[:, z0 + b:z0 + 4 * C:4], bank[4 + b][:, 0:C], 0.015625))
+        z0, written = 4 * (M + v * C), []
+        for tag, a, e_, first, deps in ([(str(i), a, b, 4 * i, [N("qy%d" % i)]) for i, (a, b) in enumerate(part)] if last and O["zsplit"] else [("", 0, C, 4, [N("qy0"), N("qy1")])]):
+            for b in range(4):
+                out = bank[first + b][:, 0:e_ - a]
+                now(N("Z%s%d" % (tag, b)), "P", deps + [N("y%d%d" % (first // 4, b)), "q_e"],
+                    mx(out, T.ec[:, 128 * b:128 * b + 128], T.es[:, 128 * b:128 * b + 128], oc_[:, a:e_], os_[:, a:e_], True, True))
+                e = eng(N("z%s%d" % (tag, b)), "S")
+                now(N("z%s%d" % (tag, b)), e, [N("Z%s%d" % (tag, b))], copy(e, T.win[:, z0 + 4 * a + b:z0 + 4 * e_:4], out, 0.015625))
+                written.append(N("z%s%d" % (tag, b)))
         scans = prev(*["s%d" % hi for lo_, hi in batches])
         compares = prev(*["c%d" % k for k in range(20)])
         now(N("own"), "V", got + scans + compares, ts(T.own[:], ls[:], -1.0, OP.mult, 256.0, OP.add))
@@ -389,14 +395,13 @@ def rank_program(g, core, T, topo):
         q = eng(name, q)
         now(name, q, deps, lambda: (S if q == "S" else Y).dma_start(out, src))
 
-    fin = O["fin"]
-    fst, fq = O.get("fst", fin), O.get("fq", fin)
+    fin, fst, fq = O["fin"], O["fst"], O["fq"]
     for i in range(len(fin) - 1):
         a, b = fin[i], fin[i + 1]
         e = eng("fg%d" % i, "SV"[i % 2])
         now("fs%d" % i, "V", [N("t0"), "k1"], scan(T.fsc[:, a:b], T.k1[:, a:b], T.ptab[:, a:b]))
         now("fo%d" % i, "V", ["fs%d" % i, "cc"], ts(T.offm[:, a // 4:b // 4], T.fsc[:, a + 3:b:4], 4.0, OP.mult, T.k0[:, 1:2], OP.add))
-        now("fg%d" % i, e, ["fo%d" % i] + [N("z%d" % b4) for b4 in range(4)], copy(e, T.mf[:, 4 * a:4 * b], T.win[:].indirect(T.offm[:, a // 4:b // 4])))
+        now("fg%d" % i, e, ["fo%d" % i] + written, copy(e, T.mf[:, 4 * a:4 * b], T.win[:].indirect(T.offm[:, a // 4:b // 4])))
     for i in range(len(fq) - 1):
         a, b = fq[i], fq[i + 1]
         now("fq%d" % i, "V", ["fg%d" % j for j in meets(a, b, fin)], quant(T.fc[:, C + a:C + b], T.fs[:, C + a:C + b], T.mf[:, 4 * a:4 * b]))
@@ -404,7 +409,8 @@ def rank_program(g, core, T, topo):
         a, b = fst[i], fst[i + 1]
         store("st_m%d" % i, ["fq%d" % j for j in meets(a, b, fq)], T.oc[:, 4 * (C + a):4 * (C + b)], T.fc[:, C + a:C + b].bitcast(dt.uint8), "Y")
     for i, (a, b) in enumerate(part):
-        now("H%d" % i, "P", back[i] + [N("y0%d" % i)], mx(bank[i][:, 0:b - a], T.wcb[:, 0:128], T.wsb[:, 0:128], T.fc[:, a:b], T.fs[:, a:b], True, True))
+        now("H%d" % i, "P", back[i] + [N("y0%d" % i)] + [x for x in written if x[:3] == "z0%d" % i],
+            mx(bank[i][:, 0:b - a], T.wcb[:, 0:128], T.wsb[:, 0:128], T.fc[:, a:b], T.fs[:, a:b], True, True))
         e = eng("h%d" % i, "S")
         now("h%d" % i, e, ["H%d" % i], copy(e, T.yo[:, a:b], bank[i][:, 0:b - a]))
     store("st_c", [back[0][0], back[1][0]], T.oc[:, 0:4 * C], T.fc[:, 0:C].bitcast(dt.uint8), "Y")

from concourse.mybir import dt, AluOpType, AxisListType, ActivationFunctionType

C, M, VISITS = 320, 512, 3
CODES, U8, BF, F32, F16, U16, I32 = "float8_e4m3fn_x4", "uint8", "bfloat16", "float32", "float16", "uint16", "int32"
RUN, SEG = 64, 65
O = {"n0": 128, "pipe": False, "cuts": ((0, 64, 128, 224, 320),) * 3, "look": (0, 128, 320),
     "fin": (0, 64, 128, 192, 256, 320, 384, 448, 512), "fq": (0, 128, 256, 384, 512), "fst": (0, 256, 512), "zsplit": 1,
     "ufirst": ((0, 0), (0, 0), (0, 0)), "batches": ((3, 4), (1, 2), (0, 0)), "split": ((1, 1), (0, 0), (1, 1))}

PLAN = """
ci0 ci4 ci2 ci1 ci3 k2a cf ca0 ca3 ca1 cb4 ca2 cb1 cb0 c64 cc1 pl1 pl2 pl3 pl0 q_u qx1 qx0 et0:S A1.0 pw0:V A0.0 sg1.0 bitz2:S sg0.0 et pw1 pw4 pw3 cm
q_pl pw2 L00.0 k11 xc.1 tab0 qa2.0 k13 qc2.0 cb2 k10 q_e3 L80 L13.0 of.0 q_pw q_e1 g3.0:S L03.0 L12.0 iota2 g2.0:V L10.0 W02.0 W12.0 W22.0 W32.0 g0.0:S
q_e0 cb3 lo2.0 q_e2 g1.0:S qb1.0 L02.0 L11.0 slot.0 k22 k2b own.0 rep.0:S k21 U11.0 qb0.0 U12.0 U10.0 y11.0:V U13.0 y12.0:S U03.0 y10.0:V U00.0 y13.0:S
U02.0 L01.0 c17.0:V c14.0:V U01.0 c19.0:V y03.0:S k23 k20 c16.0:V y02.0:S qy1.0 y00.0:S y01.0:S c3.0:V c8.0:V c18.0:V c12.0:V c13.0:V k2 c15.0:V c0.0:V
xd.0 c11.0:V c4.0:V c6.0:V c5.0:S A1.1 qy0.0 c10.0:S c9.0:S s4.0 sg1.1 A0.1 k12 c7.0:V Z2.0 cc c2.0:V Z0.0 sg0.1 o4.0 s2.0 Z1.0 z2.0:S t4.0 c1.0:S
z0.0:S qa2.1 qc2.1 t3.0 W02.1 W12.1 W22.1 o2.0 s0.0 W32.1 Z3.0 lo2.1 t2.0 z3.0:S xl2.0 o0.0 z1.0:S t1.0 xs.0 t0.0 xc.0 rep.1:S lk1.1 lk0.1 sc1.1 L13.1
own.1 L10.1 sc0.1 L11.1 of1.1 c7.1:S L12.1 c18.1:V c19.1:V c17.1:S slot.1 c15.1:S of0.1 c9.1:V g3.1:S g2.1:V L02.1 L03.1 g1.1:V g0.1:S c16.1:S qb1.1
c12.1:S c13.1:S c6.1:S c14.1:V c3.1:S c1.1:V c8.1:V qb0.1 c2.1:S U11.1 c5.1:V s4.1 U13.1 y11.1:S U10.1 U12.1 y13.1:V y10.1:S U02.1 U03.1 y12.1:V L00.1
y02.1:S U00.1 L01.1 y03.1:V U01.1 y00.1:S y01.1:S qy1.1 c11.1:S c10.1:S c0.1:S o4.1 c4.1:S qy0.1 A1.2 t4.1 sg1.2 xs.1 A0.2 s2.1 Z2.1 sg0.2 Z1.1 z2.1:S
Z0.1 qa2.2 z1.1:S qc2.2 o2.1 t3.1 W02.2 z0.1:S W12.2 W22.2 s0.1 W32.2 Z3.1 lo2.2 t2.1 z3.1:S xl2.1 o0.1 t1.1 xd.1 t0.1 rep.2:S lk0.2 lk1.2 sc0.2 own.2
L00.2 of0.2 c7.2:S c4.2:V c9.2:V sc1.2 L02.2 c14.2:S L03.2 c18.2:S c2.2:V g0.2:V g1.2:S of1.2 c17.2:S c15.2:V c13.2:V c19.2:S c12.2:V c5.2:V c16.2:V
slot.2 c6.2:V qb0.2 g3.2:S g2.2:V U03.2 U02.2 U00.2 y03.2:S L01.2 U01.2 s4.2 y00.2:S L11.2 L13.2 y02.2:S L12.2 qb1.2 y01.2:S L10.2 c1.2:S c8.2:V c0.2:V
c10.2:S o4.2 c11.2:S c3.2:S U11.2 qy0.2 U13.2 t4.2 U12.2 y11.2:S U10.2 xc.2 s2.2 y12.2:S Z03.2 Z00.2 Z01.2 y13.2:S Z02.2 t3.2 y10.2:S o2.2 s0.2 z01.2:S
t2.2 z00.2:S z03.2:S qy1.2 z02.2:S t1.2 xs.2 Z13.2 o0.2 Z11.2 z13.2:S Z10.2 t0.2 Z12.2 z11.2:S xd.2 z12.2:S fs6 z10.2:S fs4 fs2 fo6 fs7 fs5 fs1 fs0
fg6:S fo4 fo2 fs3 fo5 H0 fo1 fo0 fo7 fg2:V fg4:S fo3 fg5:V fg7:S st_c H1 fg3:V fg1:S fq3 fg0:S fq2 fq1 h0:S fq0 st_m1 h1:S st_m0 st_s3 st_s2 st_y st_s1
st_s0
""".split()
ENG = dict(x.split(":") for x in PLAN if ":" in x)


def _sb(n, d):
    return ("sbuf", [128, n], d)


SCRATCH = {
    "ut": _sb(512, BF), "uc": _sb(128, CODES), "us": _sb(128, U8),
    "xt": _sb(4 * C, BF), "s0c": _sb(C, CODES), "s0s": _sb(C, U8),
    "wcb": _sb(512, CODES), "wsb": _sb(512, U8),
    "win": _sb(4 * (M + VISITS * C), BF),
    "et": _sb(516, BF), "ec": _sb(512, CODES), "es": _sb(512, U8), "c64": _sb(128, BF),
    "plt": _sb(512, BF), "plc": _sb(128, CODES), "pls": _sb(128, U8),
    "pwt": _sb(560, BF), "pwc": _sb(140, CODES), "pws": _sb(140, U8),
    "qi": _sb(1, I32), "ci": _sb(8, I32), "cf": _sb(8, F32), "i64": _sb(64, F32), "ip4": _sb(128, BF),
    "mm": _sb(16, F32), "wr": _sb(4, F32), "wv": _sb(4, F32), "g4t": _sb(4, F32),
    "k0": _sb(32, F32), "k1": _sb(512, BF), "k2": _sb(8 * SEG, BF),
    "iota": _sb(M + VISITS * C, F32), "ptab": _sb(768, F32),
    "ls0": _sb(20, U16), "lo1": _sb(20, U16), "lo2": _sb(20, U16), "ls1": _sb(20, U16), "ls2": _sb(20, U16),
    "gg": _sb(C, F16), "gs": _sb(C, F16), "off0": _sb(80, U16), "off1": _sb(80, U16), "off2": _sb(80, U16),
    "bt": _sb(4 * C, BF), "bc": _sb(C, CODES), "bs": _sb(C, U8),
    "yt": _sb(4 * C, BF),
    "o1c": _sb(C, CODES), "o1s": _sb(C, U8), "o2c": _sb(C, CODES), "o2s": _sb(C, U8), "o3c": _sb(C, CODES), "o3s": _sb(C, U8),
    "s1c": _sb(C, CODES), "s1s": _sb(C, U8), "s2c": _sb(C, CODES), "s2s": _sb(C, U8),
    "fs": _sb(C + M, U8), "fc": _sb(C + M, CODES), "mf": _sb(4 * M, BF),
    "rep": _sb(C, BF), "own": _sb(20, F32),
    "cmp": _sb(20 * SEG, BF), "scn": _sb(20 * SEG, BF), "sco": _sb(20, U16),
    "fsc": _sb(M, F32), "offm": _sb(128, U16), "yo": _sb(C, F32),
}
for _i in range(3):
    SCRATCH.update({"bit%d" % _i: _sb(524, BF), "ba%dc" % _i: _sb(130, CODES), "ba%ds" % _i: _sb(130, U8), "bb%dc" % _i: _sb(130, CODES), "bb%ds" % _i: _sb(130, U8)})
for _i in range(8):
    SCRATCH["pb%d" % _i] = ("psum", [128, 512], F32)
REMOTE = [a + str(v) for v in (1, 2, 3) for a in ("al", "am", "ac", "ad", "as")] + ["sent"]
SEMAPHORES = REMOTE + ["z%d" % i for i in range(110)]

OP, ACT = AluOpType, ActivationFunctionType


def emit(g, T, steps, order, landed):
    qs = {"V": g.vector, "S": g.scalar, "P": g.tensor, "Y": g.sync, "G": g}
    place = {nm: i for i, nm in enumerate(order)}
    members = {}
    for nm in order:
        if steps[nm][3]:
            members.setdefault((steps[nm][3], steps[nm][0]), []).append(nm)
    head = {nm: nm for nm in order}
    heads = {}
    for (tag, q), ms in members.items():
        heads.setdefault(tag, []).append(ms[-1])
        for x in ms:
            head[x] = ms[-1]
    known = {q: set() for q in qs}
    after, waits, needed, before, done = {}, {}, set(), {}, {q: set() for q in "VSP"}
    for nm in order:
        q, deps, _, tag = steps[nm]
        ds = set()
        for d in deps:
            ds |= set(heads[d]) if d in heads else {head.get(d, d)}
        waits[nm] = []
        for d in sorted(ds, key=lambda d: (-place.get(d, 1 << 30), d)):
            if d not in known[q] and not (q == "P" and d in steps and steps[d][0] == "P"):
                assert d in landed or place[d] < place[nm], (nm, d)
                waits[nm].append(d)
                needed.add(d)
                known[q] |= after.get(d, {d})
        before[nm] = set(known[q])
        after[nm] = known[q] | {nm} | (set(members[tag, q]) if tag and head[nm] == nm else set())
        if q in done and nm[:3] not in ("ld_", "st_"):
            done[q] |= after[nm]
            after[nm] = set(done[q])
    token, last, count, stores = dict(landed), {}, {}, []
    for nm in order:
        q, _, call, tag = steps[nm]
        for d in waits[nm]:
            qs[q].wait_ge(T.sem[token[d][0]], token[d][1])
        ins = call()
        h, is_dma = head[nm], nm[:3] in ("ld_", "st_")
        if ins is None or (h not in needed and not is_dma):
            continue
        if h not in token:
            free = [x for x in last if last[x] in before[nm] and not is_dma]
            x = free[0] if free else "z%d" % len(count)
            last.pop(x, None)
            token[h] = (x, count.setdefault(x, 0))
        x, k = token[h][0], 16 if is_dma else 1
        ins.then_inc(T.sem[x], k)
        count[x] += k
        token[h] = (x, count[x])
        if nm == h and not is_dma:
            last[x] = nm
        if nm == h and is_dma and h not in needed:
            stores.append(h)
    for nm in stores:
        g.wait_ge(T.sem[token[nm][0]], token[nm][1])


def rank_program(g, core, T, topo):
    rank = T.rank_of(core)
    if rank is None:
        return
    n = len(T.cores)
    V, S, P, Y = g.vector, g.scalar, g.tensor, g.sync
    bank = [T["pb%d" % i] for i in range(8)]
    steps, order, landed, sent = {}, [], {}, [0]

    def now(name, q, deps, call, tag=None):
        steps[name] = (q, list(deps), call, tag)
        order.append(name)

    def eng(name, default):
        return ENG.get(name, default)

    def ts(out, in0, s1, op0, s2=None, op1=None):
        if op1 is None:
            return lambda: V.tensor_scalar(out, in0, s1, None, op0)
        return lambda: V.tensor_scalar(out, in0, s1, s2, op0, op1)

    def quant(c, s, tile):
        return lambda: V.quantize_mx(c, s, tile)

    def scan(out, keep, data):
        return lambda: V.tensor_tensor_scan(out, keep, data, 0.0, OP.add, OP.min)

    def act(out, in_, func, **kw):
        return lambda: S.activation(out, in_, func, **kw)

    def mx(out, wc, ws, xc, xs, start, stop):
        return lambda: P.matmul_mx(out, wc, ws, xc, xs, start, stop)

    def copy(q, out, in_, scale=None):
        if q == "S":
            return act(out, in_, ACT.Copy) if scale is None else act(out, in_, ACT.Copy, scale=scale)
        return (lambda: V.tensor_copy(out, in_)) if scale is None else ts(out, in_, scale, OP.mult)

    def send(dst, out, src, role):
        def call():
            rid, pid, _ = topo.addr(dst)
            g.remote_dma(out, src, T.sem[role], T.sem["sent"], pid, rid, topo.mask(core, dst))
            sent[0] += len(topo.engines(core, dst))
        return call

    def arrival(src, role):
        landed[role] = (role, len(topo.engines(src, core)))
        return role

    nxt, prv = T.cores[(rank + 1) % n], T.cores[(rank - 1) % n]
    home, away = T.cores[(rank - (VISITS - 1)) % n], T.cores[(rank + VISITS - 1) % n]
    n0 = O["n0"]
    part = ((0, n0), (n0, C))

    def split(src, dst, v):
        return O["split"][v][int(topo.chip(src) != topo.chip(dst))]

    now("ld_u", "S", [], lambda: S.dma_start(T.ut[:], T.u[:]))
    now("ld_x", "Y", [], lambda: Y.dma_start(T.xt[:], T.x[:]))
    now("ld_m", "Y", [], lambda: Y.dma_start(T.win[:, 0:4 * M], T.m[:]))
    now("ld_wc", "Y", [], lambda: Y.dma_start(T.wcb[:].bitcast(dt.uint8), T.wc[:]), "w")
    now("ld_ws", "Y", [], lambda: Y.dma_start(T.wsb[:], T.ws[:]), "w")

    def iota(out, pattern, base, mult):
        return lambda: g.iota(out, pattern, base, mult, allow_small_or_imprecise_dtypes=True)

    now("qi", "G", [], lambda: g.iota(T.qi[:], [[0, 1]], 0, 1))
    now("i64", "G", [], iota(T.i64[:], [[1, 64]], 0, 0))
    now("ip4", "G", [], iota(T.ip4[:], [[1, 32], [0, 4]], 0, 0))
    now("iota", "G", [], iota(T.iota[:, 0:M + C], [[1, M + C]], 0, 0))
    head = len(order)
    now("c64", "V", [], lambda: V.memset(T.c64[:], 64.0))

    def zeros(name, out, width):
        if eng(name, "S") == "S":
            now(name, "S", ["iota"], act(out, T.iota[:, 0:width], ACT.Copy, scale=0.0))
        else:
            now(name, "V", [], lambda: V.memset(out, 0.0))

    zeros("et0", T.et[:], 516)
    zeros("pw0", T.pwt[:], 560)
    zeros("bitz2", T.bit2[:, C:524], 524 - C)
    now("et", "G", ["c64", "et0"], lambda: g.affine_select(T.et[:, 3:515:4], T.c64[:], [[-1, 128]], OP.is_equal, 0.0, 0, 1))
    now("iota2", "G", [], iota(T.iota[:, M + C:M + 3 * C], [[1, 2 * C]], M + C, 0))
    now("tab0", "G", [], iota(T.ptab[:, 0:M], [[1, M]], 0, 0))

    now("ci0", "V", ["qi"], ts(T.ci[:, 0:1], T.qi[:], 15, OP.bitwise_and), "ci")
    now("ci1", "V", ["qi"], ts(T.ci[:, 1:2], T.qi[:], 3, OP.bitwise_and), "ci")
    now("ci2", "V", ["qi"], ts(T.ci[:, 2:3], T.qi[:], 2, OP.logical_shift_right, 3, OP.bitwise_and), "ci")
    now("ci3", "V", ["qi"], ts(T.ci[:, 3:4], T.qi[:], 4, OP.logical_shift_right), "ci")
    now("ci4", "V", ["qi"], ts(T.ci[:, 4:5], T.qi[:], 2, OP.logical_shift_right, 28, OP.bitwise_and), "ci")
    now("cf", "V", ["ci"], lambda: V.tensor_copy(T.cf[:, 0:5], T.ci[:, 0:5]))
    lane, l4, sel, grp, grp4 = [T.cf[:, i:i + 1] for i in range(5)]
    wgt = T.wv[:, 0:1]
    now("ca0", "V", ["cf", "i64"], ts(T.mm[:, 0:9], T.i64[:, 0:9], lane, OP.is_lt, 1.0, OP.add))
    now("ca3", "V", ["cf", "i64"], ts(T.g4t[:], T.i64[:, 0:4], grp4, OP.add))
    now("cb4", "V", ["ca0"], lambda: V.tensor_reduce(T.wr[:, 0:1], T.mm[:, 0:9], AxisListType.X, OP.mult))
    now("cc1", "V", ["cb4"], ts(wgt, lane, 9.0, OP.is_lt, T.wr[:, 0:1], OP.mult))
    for k in range(4):
        now("pl%d" % k, "V", ["cc1", "ca3", "ip4"], ts(T.plt[:, k:512:4], T.ip4[:], T.g4t[:, k:k + 1], OP.is_equal, wgt, OP.mult), "pl")
    for k in range(4):
        now("pw%d" % (k + 1), "V", ["cc1", "pw0"], ts(T.pwt[:, 48 + 5 * k:560:64], T.i64[:, 0:8], grp, OP.is_equal, wgt, OP.mult), "pw")
    now("q_u", "V", ["ld_u"], quant(T.uc[:], T.us[:], T.ut[:]))
    now("q_pl", "V", ["pl"], quant(T.plc[:], T.pls[:], T.plt[:]))
    now("q_pw", "V", ["pw"], quant(T.pwc[:], T.pws[:], T.pwt[:]))
    now("ca1", "V", ["cf"], ts(T.k0[:, 2:3], sel, 1.0, OP.add))
    now("cb0", "V", ["cf", "i64"], ts(T.k0[:, 4:8], T.i64[:, 0:4], sel, OP.is_equal, 4096.0, OP.mult))
    now("cb1", "V", ["ca1", "i64"], ts(T.k0[:, 8:12], T.i64[:, 0:4], T.k0[:, 2:3], OP.is_equal, -2048.0, OP.mult))
    now("cm", "V", ["cb0", "cb1"], lambda: V.tensor_tensor(T.k0[:, 12:16], T.k0[:, 4:8], T.k0[:, 8:12], OP.add))
    now("cb3", "V", ["cf"], ts(T.k0[:, 0:1], sel, 3.0, OP.is_lt, 8192.0, OP.mult))
    now("cc", "V", ["cb3"], ts(T.k0[:, 1:2], T.k0[:, 0:1], l4, OP.add))
    for k in range(4):
        now("k1%d" % k, "S", ["cm", "ip4"], act(T.k1[:, k:M:4], T.ip4[:], ACT.Identity, bias=T.k0[:, 12 + k:13 + k], scale=0.0), "k1")
    now("ca2", "V", ["cf", "i64"], ts(T.k0[:, 16:20], T.i64[:, 0:4], 16.0, OP.mult, lane, OP.add))
    now("cb2", "S", ["ca2"], act(T.k0[:, 20:24], T.k0[:, 16:20], ACT.Identity, bias=-0.5, scale=-1.0 / 256))
    now("k2a", "S", ["i64"], act(T.k2[:, 0:4 * SEG:SEG], T.i64[:, 0:4], ACT.Identity, bias=2.0, scale=0.0), "k2s")
    now("k2b", "S", ["i64"], act(T.k2[:, RUN:4 * SEG:SEG], T.i64[:, 0:4], ACT.Identity, bias=0.25, scale=0.0), "k2s")
    for k in range(4):
        now("k2%d" % k, "V", ["cb2"], ts(T.k2[:, SEG * k + 1:SEG * k + RUN], T.i64[:, 1:RUN], T.k0[:, 16 + k:17 + k], OP.is_equal, T.k0[:, 20 + k:21 + k], OP.mult), "k2h")
    now("k2", "S", ["k2h", "k2s"], act(T.k2[:, 4 * SEG:8 * SEG], T.k2[:, 0:4 * SEG], ACT.Copy))
    if O["pipe"]:
        for h, (a, b) in enumerate(part):
            now("bitz%d" % h, "S", ["iota"], act(T["bit%d" % h][:, b - a:524], T.iota[:, b - a:524], ACT.Copy, scale=0.0))

    def pieces(v):
        return [(0, 0, n0, [0]), (1, n0, C, [1])] if v and O["pipe"] else [(2, 0, C, [0, 1])]

    def addresses(v, sc, ss, ready):
        out = [T.ls0, T.lo1, T.lo2][v]
        for h, a0, b0, parts in pieces(v):
            bits, nm = T["bit%d" % h], (lambda x, d=0, h=h: "%s%d.%d" % (x, h, v + d))
            old = v > 0 and nm("qa", -1) in steps
            e = eng("sg%d.%d" % (parts[0], v), "S" if v else "V")
            for i in parts:
                a, b = part[i]
                now("A%d.%d" % (i, v), "P", ["q_u", ready[i]] + (["y0%d.%d" % (i, v - 1)] if v else []),
                    mx(bank[i][:, 0:b - a], T.uc[:], T.us[:], sc[:, a:b], ss[:, a:b], True, True))
                deps = ["A%d.%d" % (i, v)] + ([nm("qa", -1), nm("qc", -1)] if old else [])
                if e == "S":
                    now("sg%d.%d" % (i, v), "S", deps, act(bits[:, a - a0:b - a0], bank[i][:, 0:b - a], ACT.Sign, bias=-2.0 ** -120))
                else:
                    now("sg%d.%d" % (i, v), "V", deps, ts(bits[:, a - a0:b - a0], bank[i][:, 0:b - a], 0.0, OP.is_gt))
            deps = ["sg%d.%d" % (i, v) for i in parts] + ["bitz%d" % h] + ([nm("W3", -1)] if old else [])
            now(nm("qa"), "V", deps, quant(T["ba%dc" % h][:], T["ba%ds" % h][:], bits[:, 0:520]))
            now(nm("qc"), "V", deps, quant(T["bb%dc" % h][:], T["bb%ds" % h][:], bits[:, 4:524]))
            pb = 2 + h % 2
            for i, s in enumerate((0, 2, 1, 3)):
                bc, bs = T["b%s%dc" % ("ab"[s % 2], h)], T["b%s%ds" % ("ab"[s % 2], h)]
                a, o = 12 - 4 * s, s - s % 2
                deps = ["q_pw", nm("qa" if s % 2 == 0 else "qc")] + (["y0%d.%d" % (pb, v - 1)] if v else [])
                now(nm("W%d" % i), "P", deps, mx(bank[pb][:, 0:128], T.pwc[:, a:a + 128], T.pws[:, a:a + 128], bc[:, o:o + 128], bs[:, o:o + 128], i == 0, i == 3))
            src = bank[pb][:, 0:(b0 - a0) // 4:4]
            dst_ = out[:, a0 // 16:b0 // 16]
            now(nm("lo"), "V", [nm("W3")], ts(dst_, src, 0.5, OP.mult, 255.5, OP.add) if e == "S" else copy("V", dst_, src))

    for i, (a, b) in enumerate(part):
        now("qx%d" % i, "V", ["ld_x"], quant(T.s0c[:, a:b], T.s0s[:, a:b], T.xt[:, 4 * a:4 * b]))
    addresses(0, T.s0c, T.s0s, ["qx0", "qx1"])
    now("L80", "P", ["q_pl", "qa2.0"], mx(bank[3][:, 0:128], T.plc[:], T.pls[:], T.ba2c[:, 0:128], T.ba2s[:, 0:128], True, True))
    now("of.0", "V", ["L80", "cf"], ts(T.off0[:], bank[3][:, 0:80], 4.0, OP.mult, l4, OP.add))
    for b in range(4):
        now("q_e%d" % b, "V", ["et"], quant(T.ec[:, 128 * b:128 * b + 128], T.es[:, 128 * b:128 * b + 128], T.et[:, 3 - b:515 - b]), "q_e")

    state = [(T.s0c, T.s0s), (T.s1c, T.s1s), (T.s2c, T.s2s)]
    outs = [(T.o1c, T.o1s), (T.o2c, T.o2s), (T.o3c, T.o3s)]
    lands = [(T.s1c, T.s1s), (T.s2c, T.s2s), (T.fc, T.fs)]
    lists, sent_lists, offs = [T.ls0, T.ls1, T.ls2], [T.lo1, T.lo2], [T.off0, T.off1, T.off2]
    batches = O["batches"]

    def meets(a, b, runs):
        return [j for j in range(len(runs) - 1) if runs[j] < b and runs[j + 1] > a]

    for v in range(VISITS):
        last = v == VISITS - 1
        sc, ss = state[v]
        ls, off = lists[v], offs[v]
        oc_, os_ = outs[v]
        wlen = 4 * (M + v * C)

        def N(x, d=0):
            return "%s.%d" % (x, v + d)

        prev = (lambda *x: [N(y, -1) for y in x]) if v else (lambda *x: [])
        look, cuts = O["look"], O["cuts"][v]
        looks = [N("lk%d" % j) for j in range(len(look) - 1)] if v else []
        if v:
            came = {h: arrival(prv, "a%s%d" % ("lm"[h % 2], v)) for h, _, _, _ in pieces(v)}
            got = list(came.values())
            two = split(prv, core, v - 1)
            ready = [[arrival(prv, "ac%d" % v), arrival(prv, "as%d" % v)], [arrival(prv, ("ad%d" if two else "ac%d") % v), "as%d" % v]]
            for j in range(len(look) - 1):
                a, b = look[j], look[j + 1]
                deps = [came[h] for h, a0, b0, _ in pieces(v) if a0 < b and b0 > a]
                now(N("lk%d" % j), "V", deps + prev("t0") + (prev("sc%d" % j) if v > 1 else []), copy("V", T.gg[:, a:b], T.ptab[:, 0:M].indirect(ls[:, a // 16:b // 16])))
                now(N("sc%d" % j), "V", [N("lk%d" % j), "k1"] + (prev("of%d" % j) if v > 1 else []), scan(T.gs[:, a:b], T.k1[:, 0:b - a], T.gg[:, a:b]))
                now(N("of%d" % j), "V", [N("sc%d" % j), "cc"], ts(off[:, a // 4:b // 4], T.gs[:, a + 3:b:4], 4.0, OP.mult, T.k0[:, 1:2], OP.add))
        else:
            got = ["lo2.0"]
            ready = [["qx0", "w"], ["qx1", "w"]]
        zs = prev("z0", "z1", "z2", "z3")
        for j in range(len(cuts) - 1):
            a, b = cuts[j], cuts[j + 1]
            e = eng(N("g%d" % j), "VS"[j % 2])
            deps = [N("of%d" % k) for k in meets(a, b, look)] if v else ["of.0"]
            now(N("g%d" % j), e, deps + ["ld_m"] + zs + prev(*["qb%d" % i for i in meets(a, b, (0, n0, C))]),
                copy(e, T.bt[:, 4 * a:4 * b], T.win[:, 0:wlen].indirect(off[:, a // 4:b // 4])))
        lists_in = {2 + h % 2: N("lo%d" % h) for h, _, _, _ in pieces(v)}
        free = [[N("sg0")], [N("sg1")], [lists_in[2]], [lists_in.get(3, "of.0")] + prev("y03")] + [prev("z%d" % b) for b in range(4)]
        for i, (a, b) in enumerate(part):
            deps = [N("g%d" % j) for j in meets(a, b, cuts)] + prev(*["U%d%d" % (i, k) for k in range(4)])
            now(N("qb%d" % i), "V", deps, quant(T.bc[:, a:b], T.bs[:, a:b], T.bt[:, 4 * a:4 * b]))
            uf = bool(O["ufirst"][v][i])
            for b4 in range(4):
                w = slice(128 * b4, 128 * b4 + 128)
                out = bank[4 * i + b4][:, 0:b - a]
                un, ln = N("U%d%d" % (i, b4)), N("L%d%d" % (i, b4))
                now(ln, "P", ready[i] + ([] if uf else free[4 * i + b4]), mx(out, T.wcb[:, w], T.wsb[:, w], sc[:, a:b], ss[:, a:b], not uf, uf))
                now(un, "P", [N("qb%d" % i), "q_e"] + (free[4 * i + b4] if uf else []), mx(out, T.ec[:, w], T.es[:, w], T.bc[:, a:b], T.bs[:, a:b], uf, not uf))
                e = eng(N("y%d%d" % (i, b4)), "VVSS"[b4])
                now(N("y%d%d" % (i, b4)), e, [ln if uf else un] + prev("qy%d" % i), copy(e, T.yt[:, 4 * a + b4:4 * b:4], out, 0.015625))
            now(N("qy%d" % i), "V", [N("y%d%d" % (i, b4)) for b4 in range(4)], quant(oc_[:, a:b], os_[:, a:b], T.yt[:, 4 * a:4 * b]))
        dst = home if last else nxt
        lc, lsc = lands[v]
        if split(core, dst, v):
            now(N("xc"), "G", [N("qy0")], send(dst, lc[:, 0:n0].bitcast(dt.uint8), oc_[:, 0:n0].bitcast(dt.uint8), "ac%d" % (v + 1)))
            now(N("xd"), "G", [N("qy1")], send(dst, lc[:, n0:C].bitcast(dt.uint8), oc_[:, n0:C].bitcast(dt.uint8), "ad%d" % (v + 1)))
        else:
            now(N("xc"), "G", [], lambda: None)
            now(N("xd"), "G", [N("qy0"), N("qy1")], send(dst, lc[:, 0:C].bitcast(dt.uint8), oc_[:, 0:C].bitcast(dt.uint8), "ac%d" % (v + 1)))
        now(N("xs"), "G", [N("qy0"), N("qy1")], send(dst, lsc[:, 0:C], os_[:], "as%d" % (v + 1)))
        if not last:
            addresses(v + 1, oc_, os_, [N("qy0"), N("qy1")])
            for h, a0, b0, _ in pieces(v + 1):
                now(N("xl%d" % h), "G", [N("lo%d" % h, 1)], send(dst, lists[v + 1][:, a0 // 16:b0 // 16], sent_lists[v][:, a0 // 16:b0 // 16], "a%s%d" % ("lm"[h % 2], v + 1)))
        z0, written = 4 * (M + v * C), []
        for tag, a, e_, first, deps in ([(str(i), a, b, 4 * i, [N("qy%d" % i)]) for i, (a, b) in enumerate(part)] if last and O["zsplit"] else [("", 0, C, 4, [N("qy0"), N("qy1")])]):
            for b in range(4):
                out = bank[first + b][:, 0:e_ - a]
                now(N("Z%s%d" % (tag, b)), "P", deps + [N("y%d%d" % (first // 4, b)), "q_e"],
                    mx(out, T.ec[:, 128 * b:128 * b + 128], T.es[:, 128 * b:128 * b + 128], oc_[:, a:e_], os_[:, a:e_], True, True))
                e = eng(N("z%s%d" % (tag, b)), "S")
                now(N("z%s%d" % (tag, b)), e, [N("Z%s%d" % (tag, b))], copy(e, T.win[:, z0 + 4 * a + b:z0 + 4 * e_:4], out, 0.015625))
                written.append(N("z%s%d" % (tag, b)))
        scans = prev(*["s%d" % hi for lo_, hi in batches])
        compares = prev(*["c%d" % k for k in range(20)])
        now(N("own"), "V", got + scans + compares, ts(T.own[:], ls[:], -1.0, OP.mult, 256.0, OP.add))
        now(N("slot"), "V", got + scans, ts(T.cmp[:, RUN:20 * SEG:SEG], ls[:], -1.0 / 1024, OP.mult, 0.25, OP.add))
        e = eng(N("rep"), "S")
        now(N("rep"), e, got + ["iota"] + compares,
            act(T.rep[:], T.iota[:, 0:M].indirect(ls[:]), ACT.Identity, bias=256.0, scale=-1.0) if e == "S" else ts(T.rep[:], T.iota[:, 0:M].indirect(ls[:]), -1.0, OP.mult, 256.0, OP.add))
        for lo_, hi in batches:
            for k in range(4 * hi + 3, 4 * lo_ - 1, -1):
                e = eng(N("c%d" % k), "S")
                w, r = 16 * (k % 4 + 1) if v else RUN, RUN * (k // 4)
                out, src = T.cmp[:, SEG * k:SEG * k + w], T.rep[:, r:r + w]
                now(N("c%d" % k), e, [N("own"), N("rep")] + prev("s%d" % hi),
                    ts(out, src, T.own[:, k:k + 1], OP.not_equal) if e == "V" else act(out, src, ACT.Abs, bias=T.own[:, k:k + 1], scale=-1.0), N("cmp%d" % hi))
            a, b = 4 * SEG * lo_, 4 * SEG * (hi + 1)
            now(N("s%d" % hi), "V", [N("cmp%d" % hi), N("slot"), "k2"] + prev("o%d" % hi), scan(T.scn[:, a:b], T.k2[:, 0:b - a], T.cmp[:, a:b]))
            now(N("o%d" % hi), "V", [N("s%d" % hi)] + prev("t0"), ts(T.sco[:, 4 * lo_:4 * hi + 4], T.scn[:, a + RUN:b:SEG], -1024.0, OP.mult, 256.0, OP.add))
            for r in range(hi, lo_ - 1, -1):
                deps = [N("o%d" % hi), "iota", "iota2", "tab0"] + ([N("t%d" % (r + 1))] if r < 4 else looks)
                a = M + C * v + RUN * r
                now(N("t%d" % r), "V", deps, copy("V", T.ptab[:].indirect(T.sco[:, 4 * r:4 * r + 4]), T.iota[:, a:a + RUN]))

    two = split(away, core, VISITS - 1)
    back = [[arrival(away, "ac3"), arrival(away, "as3")], [arrival(away, "ad3" if two else "ac3"), "as3"]]

    def store(name, deps, out, src, q):
        q = eng(name, q)
        now(name, q, deps, lambda: (S if q == "S" else Y).dma_start(out, src))

    fin, fst, fq = O["fin"], O["fst"], O["fq"]
    for i in range(len(fin) - 1):
        a, b = fin[i], fin[i + 1]
        e = eng("fg%d" % i, "SV"[i % 2])
        now("fs%d" % i, "V", [N("t0"), "k1"], scan(T.fsc[:, a:b], T.k1[:, a:b], T.ptab[:, a:b]))
        now("fo%d" % i, "V", ["fs%d" % i, "cc"], ts(T.offm[:, a // 4:b // 4], T.fsc[:, a + 3:b:4], 4.0, OP.mult, T.k0[:, 1:2], OP.add))
        now("fg%d" % i, e, ["fo%d" % i] + written, copy(e, T.mf[:, 4 * a:4 * b], T.win[:].indirect(T.offm[:, a // 4:b // 4])))
    for i in range(len(fq) - 1):
        a, b = fq[i], fq[i + 1]
        now("fq%d" % i, "V", ["fg%d" % j for j in meets(a, b, fin)], quant(T.fc[:, C + a:C + b], T.fs[:, C + a:C + b], T.mf[:, 4 * a:4 * b]))
    for i in range(len(fst) - 1):
        a, b = fst[i], fst[i + 1]
        store("st_m%d" % i, ["fq%d" % j for j in meets(a, b, fq)], T.oc[:, 4 * (C + a):4 * (C + b)], T.fc[:, C + a:C + b].bitcast(dt.uint8), "Y")
    for i, (a, b) in enumerate(part):
        now("H%d" % i, "P", back[i] + [N("y0%d" % i)] + [x for x in written if x[:3] == "z0%d" % i],
            mx(bank[i][:, 0:b - a], T.wcb[:, 0:128], T.wsb[:, 0:128], T.fc[:, a:b], T.fs[:, a:b], True, True))
        e = eng("h%d" % i, "S")
        now("h%d" % i, e, ["H%d" % i], copy(e, T.yo[:, a:b], bank[i][:, 0:b - a]))
    store("st_c", [back[0][0], back[1][0]], T.oc[:, 0:4 * C], T.fc[:, 0:C].bitcast(dt.uint8), "Y")
    store("st_y", ["h0", "h1"], T.y[:], T.yo[:], "Y")
    for k in range(4):
        store("st_s%d" % k, ["as3"] + ["fq%d" % i for i in range(len(fq) - 1)], T.osc[4 * k:4 * k + 4, :], T.fs[32 * k:32 * k + 4, :], "YYSS"[k])

    plan = [x.split(":")[0] for x in PLAN]
    assert sorted(plan) == sorted(order[head:])
    emit(g, T, steps, order[:head] + plan, landed)
    g.wait_ge(T.sem["sent"], sent[0])
